import numpy as np
import ml_dtypes


def mxq(x, axis, fmt="e4m3"):
    dtype, down = {"e4m3": (ml_dtypes.float8_e4m3fn, 7), "e5m2": (ml_dtypes.float8_e5m2, 14)}[fmt]
    v = np.moveaxis(np.asarray(x, np.float32).astype(ml_dtypes.bfloat16).astype(np.float64), axis, -1)
    blocks = v.reshape(v.shape[:-1] + (-1, 32))
    amax = np.abs(blocks).max(-1, keepdims=True)
    byte = np.maximum(np.where(amax > 0, np.frexp(amax)[1] - 1 + 127, 0) - down, 1)
    scale = np.exp2(byte - 127.0)
    codes = (blocks / scale).astype(np.float32).astype(dtype).astype(np.float64)
    return np.moveaxis((codes * scale).reshape(v.shape), -1, axis)


WIDE = False


def mx_kscale(k):
    if not WIDE:
        return np.ones(k)
    levels = np.array([10, -10, 5, -5, 0])
    if k % 512:
        return np.exp2(np.random.permutation(np.resize(levels, k // 32))).repeat(32)
    a = np.empty((k // 512, 16))
    for p in range(k // 512):
        a[p, :8] = np.random.permutation(np.resize(levels, 8))
        for g in range(8):
            far = levels[np.abs(levels - a[p, g]) >= 10]
            a[p, g + 8] = far[np.random.randint(len(far))]
    return np.exp2(a.ravel()).repeat(32)


def f64(x):
    return np.asarray(x).astype(np.float64)


def striped(idx):
    return np.tile(idx.reshape(-1, 16).T, (8, 1)).astype(np.uint16)


def unstriped(offs):
    return offs[:16].T.reshape(-1).astype(np.int64)


def pack_weight(w):
    k, n = w.shape
    w = f64(np.asarray(w, np.float32).astype(ml_dtypes.bfloat16)).reshape(k // 32, 32, n)
    amax = np.abs(w).max(1)
    byte = np.clip(np.where(amax > 0, np.frexp(amax)[1] - 1 + 127 - 7, 1), 1, 254)
    scaled = (w * np.exp2(127.0 - byte)[:, None, :]).reshape(k, n).astype(np.float32)
    words = np.ascontiguousarray(scaled.reshape(k // 512, 128, 4, n).transpose(0, 1, 3, 2)).astype(ml_dtypes.float8_e4m3fn).view(np.uint8)
    return words, np.ascontiguousarray(byte.astype(np.uint8).reshape(k // 512, 16, n))


def unpack_weight(words, scales):
    g, p, n, _ = words.shape
    vals = np.ascontiguousarray(words).view(ml_dtypes.float8_e4m3fn).astype(np.float64) * np.repeat(np.exp2(scales.astype(np.float64) - 127.0), 8, axis=1)[..., None]
    return vals.transpose(0, 1, 3, 2).reshape(g * 512, n)


K, T, S, D, H, G, R = 1024, 2048, 512, 4, 512, 2048, 512
P = 2 ** 7


def setup_inputs():
    n = np.random.standard_normal
    s = mx_kscale(K)[:, None]
    u = mx_kscale(H)
    packed_xT = pack_weight(n((K, T)) * s)
    packed_vT = pack_weight(n((H, G)) / np.sqrt(H) / u[:, None])
    return {
        "x_words": packed_xT[0],
        "x_scales": packed_xT[1],
        "w1": (n((K, H)) / np.sqrt(K) / s * u).astype(np.float32),
        "norm": (np.tile(np.random.uniform(0.3, 0.7, S), (P, 1))).astype(np.float32),
        "v_words": packed_vT[0],
        "v_scales": packed_vT[1],
        "bias": (np.tile(0.5 * n(G), (P, 1))).astype(np.float32),
        "offs": striped(np.random.permutation(T)[:S]),
        "items": striped(np.random.permutation(G)[:R]),
    }


def reference(x_words, x_scales, w1, norm, v_words, v_scales, bias, offs, items):
    xq = unpack_weight(x_words, x_scales)[:, unstriped(offs)]
    y = mxq(f64(w1), 0, "e4m3").T @ xq
    ss = y.reshape(len(y), -1, D).sum(axis=2)
    z = (np.repeat(ss, D, axis=1) - y) * f64(norm)[:1]
    v_items = unpack_weight(v_words, v_scales)[:, unstriped(items)]
    sc = mxq(z, 0, "e4m3").T @ v_items
    return sc + f64(bias)[:1][:, unstriped(items)]

@@ -1,0 +1,193 @@
+from contextlib import ExitStack
+
+import concourse.mybir as mybir
+from concourse.masks import make_identity
+
+K, T, S, D, H, G, R = 1024, 2048, 512, 4, 512, 2048, 512
+FLOPS = 2 * K * H * S + 2 * H * S * R
+
+F32 = mybir.dt.float32
+BF16 = mybir.dt.bfloat16
+I32 = mybir.dt.int32
+U32 = mybir.dt.uint32
+U16 = mybir.dt.uint16
+U8 = mybir.dt.uint8
+FP8X4 = mybir.dt.float8_e4m3fn_x4
+COPY = mybir.ActivationFunctionType.Copy
+MULT = mybir.AluOpType.mult
+ADD = mybir.AluOpType.add
+
+P = 128
+PACK = 4
+V = S // D
+HALF = H // 2
+CAST_V = 128
+
+
+def tile_picked_yfism_lin_p_kernel(
+    tc, x_words, x_scales, w1, norm, v_words, v_scales, bias, offs, items, out
+):
+    nc = tc.nc
+    with ExitStack() as ctx:
+        sb = ctx.enter_context(tc.tile_pool(name="sb", bufs=1))
+        ps = ctx.enter_context(tc.psum_pool(name="ps", bufs=1))
+
+        def bank(b, name):
+            return ps.tile([P, 512], F32, name=name, tag="bank%d" % b)
+
+        def tile(shape, dtype, name):
+            return sb.tile(shape, dtype, name=name, align_bytes=64)
+
+        offs_sb = tile([P, S // 16], U16, "offs_sb")
+        items_sb = tile([P, R // 16], U16, "items_sb")
+        xs = tile([P, T], U8, "xs")
+        vs = tile([P, G], U8, "vs")
+        bias_sb = tile([P, G], F32, "bias_sb")
+        nc.vector.memset(xs[:].bitcast(I32), 0)
+        nc.vector.memset(bias_sb[:], 0.0)
+        nc.gpsimd.memset(vs[:].bitcast(I32), 0)
+        ident = tile([P, P], F32, "ident")
+        make_identity(nc, ident[:])
+
+        nc.sync.dma_start(offs_sb[:], offs)
+        nc.sync.dma_start(items_sb[:], items)
+        w0 = tile([P, PACK * H], F32, "w0")
+        nc.sync.dma_start(w0[:], w1[0:512, :].rearrange("(p j) c -> p (j c)", j=PACK))
+        for q in range(4):
+            nc.scalar.dma_start(xs[32 * q : 32 * q + 8, :].bitcast(I32), x_scales[:, 4 * q : 4 * q + 4, :].bitcast(I32))
+        nc.scalar.dma_start(bias_sb[0:1, :], bias[0:1, :])
+        xw = [tile([P, T], U32, "xw%d" % o) for o in range(2)]
+        for o in range(2):
+            nc.sync.dma_start(xw[o][:].bitcast(I32), x_words[o].rearrange("p n t -> p (n t)").bitcast(I32))
+        wh = [tile([P, PACK, HALF], F32, "wh%d" % h) for h in range(2)]
+        for h in range(2):
+            nc.sync.dma_start(wh[h][:], w1[512:1024, h * HALF : (h + 1) * HALF].rearrange("(p j) c -> p j c", j=PACK))
+        vw = tile([P, G], U32, "vw")
+        nc.sync.dma_start(vw[:].bitcast(I32), v_words[0].rearrange("p n t -> p (n t)").bitcast(I32))
+        for q in range(4):
+            nc.gpsimd.dma_start(vs[32 * q : 32 * q + 4, :].bitcast(I32), v_scales[0, 4 * q : 4 * q + 4, :].bitcast(I32))
+        nrm = tile([P, D], F32, "nrm")
+        nc.scalar.dma_start(nrm[:], norm[0, :].rearrange("(v d) -> v d", d=D))
+
+        def cast(eng_copy, dst, src):
+            eng_copy(dst.rearrange("p (c i t) -> p c t i", i=4, t=PACK), src.rearrange("p t (c i) -> p c t i", i=4))
+
+        xs_g = tile([P, S], U8, "xs_g")
+        nc.vector.tensor_copy(xs_g[:], xs[:].indirect(offs_sb[:]))
+        xs_p = tile([P, S], U8, "xs_p")
+        nc.vector.tensor_copy(
+            xs_p[:].rearrange("p (d c i) -> p c d i", d=D, i=16), xs_g[:].rearrange("p (c i d) -> p c d i", d=D, i=16)
+        )
+        bias_g = tile([P, R], F32, "bias_g")
+        nc.vector.tensor_copy(bias_g[:], bias_sb[:].indirect(items_sb[:]))
+        bt = bank(7, "bt")
+        for c in range(4):
+            nc.tensor.transpose(bt[:, c * P : (c + 1) * P], bias_g[:, c * P : (c + 1) * P], ident[:])
+        bias_col = tile([P, 4], F32, "bias_col")
+        nc.scalar.copy(bias_col[:], bt[:, 0:512:P])
+        bb = bank(5, "bb")
+        for c in range(4):
+            nc.tensor.transpose(bb[:, c * P : (c + 1) * P], bias_col[:, c : c + 1].to_broadcast([P, P]), ident[:])
+        bias_bc = tile([P, R], F32, "bias_bc")
+        nc.scalar.copy(bias_bc[:], bb[:])
+
+        w0b = tile([P, PACK * H], BF16, "w0b")
+        w0v = w0[:].rearrange("p (j c) -> p j c", j=PACK)
+        w0c = tile([P, H], U32, "w0c")
+        w0s = tile([P, H], U8, "w0s")
+        for h in range(2):
+            cast(nc.scalar.copy, w0b[:, h * 1024 : (h + 1) * 1024], w0v[:, :, h * HALF : (h + 1) * HALF])
+        nc.vector.quantize_mx(w0c[:].bitcast(FP8X4), w0s[:], w0b[:])
+
+        xp = []
+
+        def gather_x(o):
+            g = tile([P, S], U32, "xg%d" % o)
+            nc.vector.tensor_copy(g[:], xw[o][:].indirect(offs_sb[:]))
+            p = tile([P, S], U32, "xp%d" % o)
+            nc.vector.tensor_copy(
+                p[:].rearrange("p (d c i) -> p c d i", d=D, i=4), g[:].rearrange("p (c i d) -> p c d i", d=D, i=4)
+            )
+            xp.append(p)
+
+        gather_x(0)
+        vs_g = tile([P, R], U8, "vs_g")
+        nc.vector.tensor_copy(vs_g[:], vs[:].indirect(items_sb[:]))
+        order = (1, 0, 3, 2)
+        y = [[bank(4 * h + d, "y%d%d" % (h, d)) for d in range(D)] for h in range(2)]
+
+        def mm1(o, h, d, codes, scales):
+            nc.tensor.matmul_mx(
+                out=y[h][d][:, 0:HALF],
+                lhsT=xp[o][:, d * V : (d + 1) * V].bitcast(FP8X4),
+                lhsT_scale=xs_p[4 * o : P, d * V : (d + 1) * V],
+                rhs=codes.bitcast(FP8X4),
+                rhs_scale=scales,
+                start=(o == 0),
+                stop=(o == 1),
+            )
+
+        for h in range(2):
+            for d in order:
+                mm1(0, h, d, w0c[:, h * HALF : (h + 1) * HALF], w0s[:, h * HALF : (h + 1) * HALF])
+        gather_x(1)
+
+        for h in range(2):
+            wb = tile([P, PACK * HALF], BF16, "wb%d" % h)
+            cast(nc.scalar.copy, wb[:, PACK * CAST_V :], wh[h][:, :, CAST_V:])
+            cast(nc.vector.tensor_copy, wb[:, : PACK * CAST_V], wh[h][:, :, :CAST_V])
+            wc = tile([P, HALF], U32, "wc%d" % h)
+            ws = tile([P, HALF], U8, "ws%d" % h)
+            nc.vector.quantize_mx(wc[:].bitcast(FP8X4), ws[:], wb[:])
+            for d in order:
+                mm1(1, h, d, wc[:], ws[:])
+
+        z = [tile([P, H], BF16, "z%d" % d) for d in range(D)]
+        vg = tile([P, R], U32, "vg")
+        out_d = out.rearrange("(v d) g -> d v g", d=D)
+        turn_bank = (1, 3, 5, 7)
+        sc_bank = (0, 2, 4, 6)
+
+        def second(d):
+            zt = bank(turn_bank[d], "zt%d" % d)
+            words = z[d][:].bitcast(F32)
+            for u in range(2):
+                nc.tensor.transpose(zt[:, u * P : (u + 1) * P], words[:, u : 256 : 2], ident[:])
+            zq = tile([P, V * PACK], BF16, "zq%d" % d)
+            nc.scalar.copy(
+                zq[:].bitcast(F32).rearrange("p (v u) -> p v u", u=2), zt[:, 0:256].rearrange("p (u v) -> p v u", u=2)
+            )
+            zc = tile([P, V], U32, "zc%d" % d)
+            zs = tile([P, V], U8, "zs%d" % d)
+            nc.vector.quantize_mx(zc[:].bitcast(FP8X4), zs[:], zq[:])
+            sc = bank(sc_bank[d], "sc%d" % d)
+            nc.tensor.matmul_mx(
+                out=sc[:], lhsT=zc[:].bitcast(FP8X4), lhsT_scale=zs[:], rhs=vg[:].bitcast(FP8X4), rhs_scale=vs_g[:],
+                start=True, stop=True,
+            )
+            res = tile([P, R], F32, "res%d" % d)
+            nc.vector.tensor_tensor(res[:], sc[:], bias_bc[:], ADD)
+            nc.sync.dma_start(out_d[d], res[:])
+
+        for h in range(2):
+            yy = [y[h][d][:, 0:HALF] for d in range(D)]
+            pair = []
+            kept = []
+            for a in range(2):
+                c = tile([P, HALF], F32, "c%d%d" % (h, a))
+                nc.scalar.copy(c[:], yy[2 * a + 1])
+                s = tile([P, HALF], F32, "s%d%d" % (h, a))
+                nc.vector.tensor_tensor(s[:], yy[2 * a], c[:], ADD)
+                pair.append(s)
+                kept.append(c)
+            for d in range(D):
+                mate = kept[d // 2][:] if d % 2 == 0 else yy[d - 1]
+                m = tile([P, HALF], F32, "m%d%d" % (h, d))
+                nc.scalar.activation(m[:], mate, COPY, scale=nrm[:, d : d + 1])
+                nc.vector.scalar_tensor_tensor(
+                    z[d][:, h * HALF : (h + 1) * HALF], pair[1 - d // 2][:], nrm[:, d : d + 1], m[:], MULT, ADD
+                )
+                if h == 1 and d == 1:
+                    nc.vector.tensor_copy(vg[:], vw[:].indirect(items_sb[:]))
+        for d in range(D):
+            second(d)

@@ -21,7 +21,7 @@ P = 128
 PACK = 4
 V = S // D
 HALF = H // 2
-CAST_V = 128
+CAST_V = (128, 256)
 
 
 def tile_picked_yfism_lin_p_kernel(
@@ -43,19 +43,24 @@ def tile_picked_yfism_lin_p_kernel(
         xs = tile([P, T], U8, "xs")
         vs = tile([P, G], U8, "vs")
         bias_sb = tile([P, G], F32, "bias_sb")
-        nc.vector.memset(xs[:].bitcast(I32), 0)
-        nc.vector.memset(bias_sb[:], 0.0)
-        nc.gpsimd.memset(vs[:].bitcast(I32), 0)
+        nc.gpsimd.memset(xs[:].bitcast(I32), 0)
+        nc.vector.memset(bias_sb[0 : P - 1, :], 0.0)
+        nc.gpsimd.memset(vs[0 : P - 16, :].bitcast(I32), 0)
+        vs_p = tile([P, R], U8, "vs_p")
+        nc.gpsimd.memset(vs_p[:].bitcast(I32), 0)
         ident = tile([P, P], F32, "ident")
         make_identity(nc, ident[:])
 
         nc.sync.dma_start(offs_sb[:], offs)
         nc.sync.dma_start(items_sb[:], items)
+        nc.scalar.dma_start(bias_sb[P - 1 : P, :], bias[0:1, :])
+        nc.scalar.dma_start(vs[P - 16 : P, :].bitcast(I32), v_scales[0].bitcast(I32))
+        nrm = tile([P, D], F32, "nrm")
+        nc.scalar.dma_start(nrm[:], norm[0, :].rearrange("(v d) -> v d", d=D))
         w0 = tile([P, PACK * H], F32, "w0")
         nc.sync.dma_start(w0[:], w1[0:512, :].rearrange("(p j) c -> p (j c)", j=PACK))
         for q in range(4):
-            nc.scalar.dma_start(xs[32 * q : 32 * q + 8, :].bitcast(I32), x_scales[:, 4 * q : 4 * q + 4, :].bitcast(I32))
-        nc.scalar.dma_start(bias_sb[0:1, :], bias[0:1, :])
+            nc.sync.dma_start(xs[32 * q : 32 * q + 8, :].bitcast(I32), x_scales[:, 4 * q : 4 * q + 4, :].bitcast(I32))
         xw = [tile([P, T], U32, "xw%d" % o) for o in range(2)]
         for o in range(2):
             nc.sync.dma_start(xw[o][:].bitcast(I32), x_words[o].rearrange("p n t -> p (n t)").bitcast(I32))
@@ -64,33 +69,34 @@ def tile_picked_yfism_lin_p_kernel(
             nc.sync.dma_start(wh[h][:], w1[512:1024, h * HALF : (h + 1) * HALF].rearrange("(p j) c -> p j c", j=PACK))
         vw = tile([P, G], U32, "vw")
         nc.sync.dma_start(vw[:].bitcast(I32), v_words[0].rearrange("p n t -> p (n t)").bitcast(I32))
-        for q in range(4):
-            nc.gpsimd.dma_start(vs[32 * q : 32 * q + 4, :].bitcast(I32), v_scales[0, 4 * q : 4 * q + 4, :].bitcast(I32))
-        nrm = tile([P, D], F32, "nrm")
-        nc.scalar.dma_start(nrm[:], norm[0, :].rearrange("(v d) -> v d", d=D))
 
         def cast(eng_copy, dst, src):
             eng_copy(dst.rearrange("p (c i t) -> p c t i", i=4, t=PACK), src.rearrange("p t (c i) -> p c t i", i=4))
 
-        xs_g = tile([P, S], U8, "xs_g")
-        nc.vector.tensor_copy(xs_g[:], xs[:].indirect(offs_sb[:]))
-        xs_p = tile([P, S], U8, "xs_p")
-        nc.vector.tensor_copy(
-            xs_p[:].rearrange("p (d c i) -> p c d i", d=D, i=16), xs_g[:].rearrange("p (c i d) -> p c d i", d=D, i=16)
-        )
+        vs_g = tile([P, R], U8, "vs_g")
         bias_g = tile([P, R], F32, "bias_g")
         nc.vector.tensor_copy(bias_g[:], bias_sb[:].indirect(items_sb[:]))
         bt = bank(7, "bt")
         for c in range(4):
             nc.tensor.transpose(bt[:, c * P : (c + 1) * P], bias_g[:, c * P : (c + 1) * P], ident[:])
         bias_col = tile([P, 4], F32, "bias_col")
-        nc.scalar.copy(bias_col[:], bt[:, 0:512:P])
+        nc.scalar.copy(bias_col[:], bt[:, P - 1 : 512 : P])
         bb = bank(5, "bb")
         for c in range(4):
             nc.tensor.transpose(bb[:, c * P : (c + 1) * P], bias_col[:, c : c + 1].to_broadcast([P, P]), ident[:])
         bias_bc = tile([P, R], F32, "bias_bc")
         nc.scalar.copy(bias_bc[:], bb[:])
 
+        nc.vector.tensor_copy(vs_g[:], vs[:].indirect(items_sb[:]))
+        for q in range(4):
+            rows = slice(P - 16 + 4 * q, P - 12 + 4 * q)
+            nc.sync.dma_start(vs_p[32 * q : 32 * q + 4, :].bitcast(I32), vs_g[rows, :].bitcast(I32))
+        xs_g = tile([P, S], U8, "xs_g")
+        nc.vector.tensor_copy(xs_g[:], xs[:].indirect(offs_sb[:]))
+        xs_p = tile([P, S], U8, "xs_p")
+        nc.vector.tensor_copy(
+            xs_p[:].rearrange("p (d c i) -> p c d i", d=D, i=16), xs_g[:].rearrange("p (c i d) -> p c d i", d=D, i=16)
+        )
         w0b = tile([P, PACK * H], BF16, "w0b")
         w0v = w0[:].rearrange("p (j c) -> p j c", j=PACK)
         w0c = tile([P, H], U32, "w0c")
@@ -111,8 +117,6 @@ def tile_picked_yfism_lin_p_kernel(
             xp.append(p)
 
         gather_x(0)
-        vs_g = tile([P, R], U8, "vs_g")
-        nc.vector.tensor_copy(vs_g[:], vs[:].indirect(items_sb[:]))
         order = (1, 0, 3, 2)
         y = [[bank(4 * h + d, "y%d%d" % (h, d)) for d in range(D)] for h in range(2)]
 
@@ -134,8 +138,10 @@ def tile_picked_yfism_lin_p_kernel(
 
         for h in range(2):
             wb = tile([P, PACK * HALF], BF16, "wb%d" % h)
-            cast(nc.scalar.copy, wb[:, PACK * CAST_V :], wh[h][:, :, CAST_V:])
-            cast(nc.vector.tensor_copy, wb[:, : PACK * CAST_V], wh[h][:, :, :CAST_V])
+            cv = CAST_V[h]
+            if cv < HALF:
+                cast(nc.scalar.copy, wb[:, PACK * cv :], wh[h][:, :, cv:])
+            cast(nc.vector.tensor_copy, wb[:, : PACK * cv], wh[h][:, :, :cv])
             wc = tile([P, HALF], U32, "wc%d" % h)
             ws = tile([P, HALF], U8, "ws%d" % h)
             nc.vector.quantize_mx(wc[:].bitcast(FP8X4), ws[:], wb[:])
@@ -145,8 +151,8 @@ def tile_picked_yfism_lin_p_kernel(
         z = [tile([P, H], BF16, "z%d" % d) for d in range(D)]
         vg = tile([P, R], U32, "vg")
         out_d = out.rearrange("(v d) g -> d v g", d=D)
-        turn_bank = (1, 3, 5, 7)
-        sc_bank = (0, 2, 4, 6)
+        turn_bank = (3, 7, 1, 5)
+        sc_bank = (2, 4, 0, 6)
 
         def second(d):
             zt = bank(turn_bank[d], "zt%d" % d)
@@ -162,7 +168,7 @@ def tile_picked_yfism_lin_p_kernel(
             nc.vector.quantize_mx(zc[:].bitcast(FP8X4), zs[:], zq[:])
             sc = bank(sc_bank[d], "sc%d" % d)
             nc.tensor.matmul_mx(
-                out=sc[:], lhsT=zc[:].bitcast(FP8X4), lhsT_scale=zs[:], rhs=vg[:].bitcast(FP8X4), rhs_scale=vs_g[:],
+                out=sc[:], lhsT=zc[:].bitcast(FP8X4), lhsT_scale=zs[:], rhs=vg[:].bitcast(FP8X4), rhs_scale=vs_p[:],
                 start=True, stop=True,
             )
             res = tile([P, R], F32, "res%d" % d)
@@ -180,14 +186,14 @@ def tile_picked_yfism_lin_p_kernel(
                 nc.vector.tensor_tensor(s[:], yy[2 * a], c[:], ADD)
                 pair.append(s)
                 kept.append(c)
-            for d in range(D):
+            if h == 1:
+                nc.vector.tensor_copy(vg[:], vw[:].indirect(items_sb[:]))
+            for d in (2, 0, 3, 1):
                 mate = kept[d // 2][:] if d % 2 == 0 else yy[d - 1]
                 m = tile([P, HALF], F32, "m%d%d" % (h, d))
                 nc.scalar.activation(m[:], mate, COPY, scale=nrm[:, d : d + 1])
                 nc.vector.scalar_tensor_tensor(
                     z[d][:, h * HALF : (h + 1) * HALF], pair[1 - d // 2][:], nrm[:, d : d + 1], m[:], MULT, ADD
                 )
-                if h == 1 and d == 1:
-                    nc.vector.tensor_copy(vg[:], vw[:].indirect(items_sb[:]))
-        for d in range(D):
-            second(d)
+                if h == 1:
+                    second(d)

@@ -35,8 +35,8 @@ def tile_picked_yfism_lin_p_kernel(
         def bank(b, name):
             return ps.tile([P, 512], F32, name=name, tag="bank%d" % b)
 
-        def tile(shape, dtype, name):
-            return sb.tile(shape, dtype, name=name, align_bytes=64)
+        def tile(shape, dtype, name, tag=None):
+            return sb.tile(shape, dtype, name=name, tag=tag or name, align_bytes=64)
 
         offs_sb = tile([P, S // 16], U16, "offs_sb")
         items_sb = tile([P, R // 16], U16, "items_sb")
@@ -56,7 +56,6 @@ def tile_picked_yfism_lin_p_kernel(
         nc.scalar.dma_start(bias_sb[P - 1 : P, :], bias[0:1, :])
         nc.scalar.dma_start(vs[P - 16 : P, :].bitcast(I32), v_scales[0].bitcast(I32))
         nrm = tile([P, D], F32, "nrm")
-        nc.scalar.dma_start(nrm[:], norm[0, :].rearrange("(v d) -> v d", d=D))
         w0 = tile([P, PACK * H], F32, "w0")
         nc.sync.dma_start(w0[:], w1[0:512, :].rearrange("(p j) c -> p (j c)", j=PACK))
         for q in range(4):
@@ -64,6 +63,7 @@ def tile_picked_yfism_lin_p_kernel(
         xw = [tile([P, T], U32, "xw%d" % o) for o in range(2)]
         for o in range(2):
             nc.sync.dma_start(xw[o][:].bitcast(I32), x_words[o].rearrange("p n t -> p (n t)").bitcast(I32))
+        nc.scalar.dma_start(nrm[:], norm[0, :].rearrange("(v d) -> v d", d=D))
         wh = [tile([P, PACK, HALF], F32, "wh%d" % h) for h in range(2)]
         for h in range(2):
             nc.sync.dma_start(wh[h][:], w1[512:1024, h * HALF : (h + 1) * HALF].rearrange("(p j) c -> p j c", j=PACK))
@@ -79,24 +79,12 @@ def tile_picked_yfism_lin_p_kernel(
         bt = bank(7, "bt")
         for c in range(4):
             nc.tensor.transpose(bt[:, c * P : (c + 1) * P], bias_g[:, c * P : (c + 1) * P], ident[:])
-        bias_col = tile([P, 4], F32, "bias_col")
-        nc.scalar.copy(bias_col[:], bt[:, P - 1 : 512 : P])
-        bb = bank(5, "bb")
-        for c in range(4):
-            nc.tensor.transpose(bb[:, c * P : (c + 1) * P], bias_col[:, c : c + 1].to_broadcast([P, P]), ident[:])
-        bias_bc = tile([P, R], F32, "bias_bc")
-        nc.scalar.copy(bias_bc[:], bb[:])
-
         nc.vector.tensor_copy(vs_g[:], vs[:].indirect(items_sb[:]))
         for q in range(4):
             rows = slice(P - 16 + 4 * q, P - 12 + 4 * q)
             nc.sync.dma_start(vs_p[32 * q : 32 * q + 4, :].bitcast(I32), vs_g[rows, :].bitcast(I32))
         xs_g = tile([P, S], U8, "xs_g")
         nc.vector.tensor_copy(xs_g[:], xs[:].indirect(offs_sb[:]))
-        xs_p = tile([P, S], U8, "xs_p")
-        nc.vector.tensor_copy(
-            xs_p[:].rearrange("p (d c i) -> p c d i", d=D, i=16), xs_g[:].rearrange("p (c i d) -> p c d i", d=D, i=16)
-        )
         w0b = tile([P, PACK * H], BF16, "w0b")
         w0v = w0[:].rearrange("p (j c) -> p j c", j=PACK)
         w0c = tile([P, H], U32, "w0c")
@@ -105,36 +93,32 @@ def tile_picked_yfism_lin_p_kernel(
             cast(nc.scalar.copy, w0b[:, h * 1024 : (h + 1) * 1024], w0v[:, :, h * HALF : (h + 1) * HALF])
         nc.vector.quantize_mx(w0c[:].bitcast(FP8X4), w0s[:], w0b[:])
 
-        xp = []
+        bias_col = tile([P, 4], F32, "bias_col", tag="w0")
+        nc.scalar.copy(bias_col[:], bt[:, P - 1 : 512 : P])
+        bb = bank(5, "bb")
+        for c in range(4):
+            nc.tensor.transpose(bb[:, c * P : (c + 1) * P], bias_col[:, c : c + 1].to_broadcast([P, P]), ident[:])
+        bias_bc = tile([P, R], F32, "bias_bc")
+        nc.scalar.copy(bias_bc[:], bb[:])
 
-        def gather_x(o):
-            g = tile([P, S], U32, "xg%d" % o)
-            nc.vector.tensor_copy(g[:], xw[o][:].indirect(offs_sb[:]))
-            p = tile([P, S], U32, "xp%d" % o)
-            nc.vector.tensor_copy(
-                p[:].rearrange("p (d c i) -> p c d i", d=D, i=4), g[:].rearrange("p (c i d) -> p c d i", d=D, i=4)
-            )
-            xp.append(p)
+        xg = [tile([P, S], U32, "xg%d" % o) for o in range(2)]
+        y = [bank(m, "y%d" % m) for m in range(4)]
 
-        gather_x(0)
-        order = (1, 0, 3, 2)
-        y = [[bank(4 * h + d, "y%d%d" % (h, d)) for d in range(D)] for h in range(2)]
-
-        def mm1(o, h, d, codes, scales):
+        def mm1(o, m, codes, scales):
             nc.tensor.matmul_mx(
-                out=y[h][d][:, 0:HALF],
-                lhsT=xp[o][:, d * V : (d + 1) * V].bitcast(FP8X4),
-                lhsT_scale=xs_p[4 * o : P, d * V : (d + 1) * V],
-                rhs=codes.bitcast(FP8X4),
-                rhs_scale=scales,
+                out=y[m][:],
+                lhsT=codes.bitcast(FP8X4),
+                lhsT_scale=scales,
+                rhs=xg[o][:].bitcast(FP8X4),
+                rhs_scale=xs_g[4 * o : P, :],
                 start=(o == 0),
                 stop=(o == 1),
             )
 
-        for h in range(2):
-            for d in order:
-                mm1(0, h, d, w0c[:, h * HALF : (h + 1) * HALF], w0s[:, h * HALF : (h + 1) * HALF])
-        gather_x(1)
+        nc.vector.tensor_copy(xg[0][:], xw[0][:].indirect(offs_sb[:]))
+        for m in range(4):
+            mm1(0, m, w0c[:, m * P : (m + 1) * P], w0s[:, m * P : (m + 1) * P])
+        nc.vector.tensor_copy(xg[1][:], xw[1][:].indirect(offs_sb[:]))
 
         for h in range(2):
             wb = tile([P, PACK * HALF], BF16, "wb%d" % h)
@@ -145,24 +129,29 @@ def tile_picked_yfism_lin_p_kernel(
             wc = tile([P, HALF], U32, "wc%d" % h)
             ws = tile([P, HALF], U8, "ws%d" % h)
             nc.vector.quantize_mx(wc[:].bitcast(FP8X4), ws[:], wb[:])
-            for d in order:
-                mm1(1, h, d, wc[:], ws[:])
+            for m in range(2):
+                mm1(1, 2 * h + m, wc[:, m * P : (m + 1) * P], ws[:, m * P : (m + 1) * P])
 
         z = [tile([P, H], BF16, "z%d" % d) for d in range(D)]
-        vg = tile([P, R], U32, "vg")
         out_d = out.rearrange("(v d) g -> d v g", d=D)
-        turn_bank = (3, 7, 1, 5)
-        sc_bank = (2, 4, 0, 6)
+        zqs = {}
+        scs = {}
+        turn_bank = (0, 1, 2, 3)
+        sc_bank = (4, 5, 6, 7)
 
-        def second(d):
+        def turn(d):
             zt = bank(turn_bank[d], "zt%d" % d)
             words = z[d][:].bitcast(F32)
             for u in range(2):
-                nc.tensor.transpose(zt[:, u * P : (u + 1) * P], words[:, u : 256 : 2], ident[:])
+                nc.tensor.transpose(zt[:, u * P : (u + 1) * P], words[:, u * P : (u + 1) * P], ident[:])
             zq = tile([P, V * PACK], BF16, "zq%d" % d)
             nc.scalar.copy(
                 zq[:].bitcast(F32).rearrange("p (v u) -> p v u", u=2), zt[:, 0:256].rearrange("p (u v) -> p v u", u=2)
             )
+            zqs[d] = zq
+
+        def score(d):
+            zq = zqs[d]
             zc = tile([P, V], U32, "zc%d" % d)
             zs = tile([P, V], U8, "zs%d" % d)
             nc.vector.quantize_mx(zc[:].bitcast(FP8X4), zs[:], zq[:])
@@ -171,29 +160,41 @@ def tile_picked_yfism_lin_p_kernel(
                 out=sc[:], lhsT=zc[:].bitcast(FP8X4), lhsT_scale=zs[:], rhs=vg[:].bitcast(FP8X4), rhs_scale=vs_p[:],
                 start=True, stop=True,
             )
+            scs[d] = sc
+
+        def finish(d):
+            sc = scs[d]
             res = tile([P, R], F32, "res%d" % d)
             nc.vector.tensor_tensor(res[:], sc[:], bias_bc[:], ADD)
             nc.sync.dma_start(out_d[d], res[:])
 
-        for h in range(2):
-            yy = [y[h][d][:, 0:HALF] for d in range(D)]
-            pair = []
-            kept = []
-            for a in range(2):
-                c = tile([P, HALF], F32, "c%d%d" % (h, a))
-                nc.scalar.copy(c[:], yy[2 * a + 1])
-                s = tile([P, HALF], F32, "s%d%d" % (h, a))
-                nc.vector.tensor_tensor(s[:], yy[2 * a], c[:], ADD)
-                pair.append(s)
-                kept.append(c)
-            if h == 1:
-                nc.vector.tensor_copy(vg[:], vw[:].indirect(items_sb[:]))
-            for d in (2, 0, 3, 1):
-                mate = kept[d // 2][:] if d % 2 == 0 else yy[d - 1]
-                m = tile([P, HALF], F32, "m%d%d" % (h, d))
-                nc.scalar.activation(m[:], mate, COPY, scale=nrm[:, d : d + 1])
-                nc.vector.scalar_tensor_tensor(
-                    z[d][:, h * HALF : (h + 1) * HALF], pair[1 - d // 2][:], nrm[:, d : d + 1], m[:], MULT, ADD
+        rest = [bank(4 + d, "rest%d" % d) for d in range(D)]
+        for m in range(4):
+            ys = tile([P, D, V], F32, "ys%d" % m)
+            pair = tile([P, 2, V], F32, "pair%d" % m)
+            if m == 3:
+                nc.vector.tensor_reduce(
+                    pair[:], y[m][:].rearrange("p (v a e) -> p a v e", a=2, e=2), mybir.AxisListType.X, ADD
                 )
-                if h == 1:
-                    second(d)
+            nc.scalar.copy(ys[:], y[m][:].rearrange("p (v d) -> p d v", d=D))
+            if m < 3:
+                nc.vector.tensor_tensor(pair[:], ys[:, 0:D:2, :], ys[:, 1:D:2, :], ADD)
+            for d in range(D):
+                cols = rest[d][:, m * P : (m + 1) * P]
+                nc.tensor.matmul(cols, pair[:, 1 - d // 2, :], ident[:], is_transpose=True, start=True, stop=False)
+                nc.tensor.matmul(cols, ys[:, d ^ 1, :], ident[:], is_transpose=True, start=False, stop=True)
+        for d in range(D):
+            dst = z[d][:].rearrange("v (u p e) -> v u p e", u=2, e=2)
+            src = rest[d][:].rearrange("v (p u e) -> v u p e", u=2, e=2)
+            if d % 2 == 0:
+                nc.scalar.activation(dst, src, COPY, scale=nrm[:, d : d + 1])
+            else:
+                nc.vector.tensor_scalar(dst, src, nrm[:, d : d + 1], None, MULT)
+        for d in range(D):
+            turn(d)
+        vg = tile([P, R], U32, "vg", tag="pair1")
+        nc.vector.tensor_copy(vg[:], vw[:].indirect(items_sb[:]))
+        for d in range(D):
+            score(d)
+        for d in range(D):
+            finish(d)

@@ -19,9 +19,7 @@ ADD = mybir.AluOpType.add
 
 P = 128
 PACK = 4
-V = S // D
-HALF = H // 2
-CAST_V = (128, 256)
+HALF = S // 2
 
 
 def tile_picked_yfism_lin_p_kernel(
@@ -43,8 +41,10 @@ def tile_picked_yfism_lin_p_kernel(
         xs = tile([P, T], U8, "xs")
         vs = tile([P, G], U8, "vs")
         bias_sb = tile([P, G], F32, "bias_sb")
-        nc.gpsimd.memset(xs[:].bitcast(I32), 0)
+        nc.gpsimd.memset(xs[0 : P - 32, :].bitcast(I32), 0)
         nc.vector.memset(bias_sb[0 : P - 1, :], 0.0)
+        xs_p = tile([P, S], U8, "xs_p")
+        nc.gpsimd.memset(xs_p[:].bitcast(I32), 0)
         nc.gpsimd.memset(vs[0 : P - 16, :].bitcast(I32), 0)
         vs_p = tile([P, R], U8, "vs_p")
         nc.gpsimd.memset(vs_p[:].bitcast(I32), 0)
@@ -52,149 +52,164 @@ def tile_picked_yfism_lin_p_kernel(
         make_identity(nc, ident[:])
 
         nc.sync.dma_start(offs_sb[:], offs)
+        nc.scalar.dma_start(xs[P - 32 : P, :].bitcast(I32), x_scales.rearrange("o q n -> (o q) n").bitcast(I32))
         nc.sync.dma_start(items_sb[:], items)
-        nc.scalar.dma_start(bias_sb[P - 1 : P, :], bias[0:1, :])
         nc.scalar.dma_start(vs[P - 16 : P, :].bitcast(I32), v_scales[0].bitcast(I32))
-        nrm = tile([P, D], F32, "nrm")
-        w0 = tile([P, PACK * H], F32, "w0")
-        nc.sync.dma_start(w0[:], w1[0:512, :].rearrange("(p j) c -> p (j c)", j=PACK))
-        for q in range(4):
-            nc.sync.dma_start(xs[32 * q : 32 * q + 8, :].bitcast(I32), x_scales[:, 4 * q : 4 * q + 4, :].bitcast(I32))
-        xw = [tile([P, T], U32, "xw%d" % o) for o in range(2)]
+        nc.scalar.dma_start(bias_sb[P - 1 : P, :], bias[0:1, :])
+        nrm = tile([P, 2, 2], F32, "nrm")
+        nc.scalar.dma_start(nrm[:], norm[0, :].rearrange("(h c e) -> c h e", h=2, e=2))
+        wf = [tile([P, PACK * H], F32, "wf%d" % o) for o in range(2)]
         for o in range(2):
-            nc.sync.dma_start(xw[o][:].bitcast(I32), x_words[o].rearrange("p n t -> p (n t)").bitcast(I32))
-        nc.scalar.dma_start(nrm[:], norm[0, :].rearrange("(v d) -> v d", d=D))
-        wh = [tile([P, PACK, HALF], F32, "wh%d" % h) for h in range(2)]
-        for h in range(2):
-            nc.sync.dma_start(wh[h][:], w1[512:1024, h * HALF : (h + 1) * HALF].rearrange("(p j) c -> p j c", j=PACK))
-        vw = tile([P, G], U32, "vw")
-        nc.sync.dma_start(vw[:].bitcast(I32), v_words[0].rearrange("p n t -> p (n t)").bitcast(I32))
+            nc.sync.dma_start(wf[o][:], w1[512 * o : 512 * (o + 1), :].rearrange("(p j) c -> p (j c)", j=PACK))
+
+        xs_g = tile([P, S], U8, "xs_g")
+        nc.vector.tensor_copy(xs_g[:], xs[:].indirect(offs_sb[:]))
+        vs_g = tile([P, R], U8, "vs_g")
+        nc.vector.tensor_copy(vs_g[:], vs[:].indirect(items_sb[:]))
+        bias_g = tile([P, R], F32, "bias_g")
+        nc.vector.tensor_copy(bias_g[:], bias_sb[:].indirect(items_sb[:]))
+
+        def place(plane, first, gathered, row):
+            nc.sync.dma_start(plane[first : first + 4, :].bitcast(I32), gathered[row : row + 4, :].bitcast(I32))
+
+        def load_words(name, tag, words):
+            window = tile([P, T], U32, name, tag=tag)
+            nc.sync.dma_start(window[:].bitcast(I32), words.rearrange("p n t -> p (n t)").bitcast(I32))
+            return window
+
+        moves = [(32 * q + 4 * o, P - 32 + 16 * o + 4 * q) for o in range(2) for q in range(4)]
+        for first, row in moves[:4]:
+            place(xs_p, first, xs_g, row)
+        xw = [load_words("xw0", "xs", x_words[0])]
+        for first, row in moves[4:]:
+            place(xs_p, first, xs_g, row)
+        xw.append(load_words("xw1", "vs", x_words[1]))
+        vw = load_words("vw", "bias_sb", v_words[0])
+        for q in range(4):
+            place(vs_p, 32 * q, vs_g, P - 16 + 4 * q)
 
         def cast(eng_copy, dst, src):
             eng_copy(dst.rearrange("p (c i t) -> p c t i", i=4, t=PACK), src.rearrange("p t (c i) -> p c t i", i=4))
 
-        vs_g = tile([P, R], U8, "vs_g")
-        bias_g = tile([P, R], F32, "bias_g")
-        nc.vector.tensor_copy(bias_g[:], bias_sb[:].indirect(items_sb[:]))
         bt = bank(7, "bt")
         for c in range(4):
             nc.tensor.transpose(bt[:, c * P : (c + 1) * P], bias_g[:, c * P : (c + 1) * P], ident[:])
-        nc.vector.tensor_copy(vs_g[:], vs[:].indirect(items_sb[:]))
-        for q in range(4):
-            rows = slice(P - 16 + 4 * q, P - 12 + 4 * q)
-            nc.sync.dma_start(vs_p[32 * q : 32 * q + 4, :].bitcast(I32), vs_g[rows, :].bitcast(I32))
-        xs_g = tile([P, S], U8, "xs_g")
-        nc.vector.tensor_copy(xs_g[:], xs[:].indirect(offs_sb[:]))
-        w0b = tile([P, PACK * H], BF16, "w0b")
-        w0v = w0[:].rearrange("p (j c) -> p j c", j=PACK)
-        w0c = tile([P, H], U32, "w0c")
-        w0s = tile([P, H], U8, "w0s")
-        for h in range(2):
-            cast(nc.scalar.copy, w0b[:, h * 1024 : (h + 1) * 1024], w0v[:, :, h * HALF : (h + 1) * HALF])
-        nc.vector.quantize_mx(w0c[:].bitcast(FP8X4), w0s[:], w0b[:])
 
-        bias_col = tile([P, 4], F32, "bias_col", tag="w0")
+        wc = [tile([P, H], U32, "wc%d" % o) for o in range(2)]
+        ws = [tile([P, H], U8, "ws%d" % o) for o in range(2)]
+
+        def quant_w(o, casts):
+            wb = tile([P, PACK * H], BF16, "wb%d" % o)
+            wv = wf[o][:].rearrange("p (j c) -> p j c", j=PACK)
+            for h in range(2):
+                cast(casts[h], wb[:, h * 1024 : (h + 1) * 1024], wv[:, :, h * 256 : (h + 1) * 256])
+            nc.vector.quantize_mx(wc[o][:].bitcast(FP8X4), ws[o][:], wb[:])
+
+        quant_w(0, (nc.scalar.copy, nc.scalar.copy))
+
+        bias_col = tile([P, 4], F32, "bias_col", tag="wf0")
         nc.scalar.copy(bias_col[:], bt[:, P - 1 : 512 : P])
-        bb = bank(5, "bb")
+        bb = bank(6, "bb")
         for c in range(4):
             nc.tensor.transpose(bb[:, c * P : (c + 1) * P], bias_col[:, c : c + 1].to_broadcast([P, P]), ident[:])
         bias_bc = tile([P, R], F32, "bias_bc")
+
+        quant_w(1, (nc.scalar.copy, nc.vector.tensor_copy))
         nc.scalar.copy(bias_bc[:], bb[:])
 
-        xg = [tile([P, S], U32, "xg%d" % o) for o in range(2)]
-        y = [bank(m, "y%d" % m) for m in range(4)]
+        y = [[bank(4 * h + m, "y%d%d" % (h, m)) for m in range(4)] for h in range(2)]
 
-        def mm1(o, m, codes, scales):
+        def mm1(o, h, m, xg):
             nc.tensor.matmul_mx(
-                out=y[m][:],
-                lhsT=codes.bitcast(FP8X4),
-                lhsT_scale=scales,
-                rhs=xg[o][:].bitcast(FP8X4),
-                rhs_scale=xs_g[4 * o : P, :],
+                out=y[h][m][:, 0:HALF],
+                lhsT=wc[o][:, m * P : (m + 1) * P].bitcast(FP8X4),
+                lhsT_scale=ws[o][:, m * P : (m + 1) * P],
+                rhs=xg.bitcast(FP8X4),
+                rhs_scale=xs_p[4 * o : P, h * HALF : (h + 1) * HALF],
                 start=(o == 0),
                 stop=(o == 1),
             )
 
-        nc.vector.tensor_copy(xg[0][:], xw[0][:].indirect(offs_sb[:]))
-        for m in range(4):
-            mm1(0, m, w0c[:, m * P : (m + 1) * P], w0s[:, m * P : (m + 1) * P])
-        nc.vector.tensor_copy(xg[1][:], xw[1][:].indirect(offs_sb[:]))
+        for o in range(2):
+            for h in range(2):
+                xg = tile([P, HALF], U32, "xg%d%d" % (o, h))
+                nc.vector.tensor_copy(xg[:], xw[o][:].indirect(offs_sb[:, 16 * h : 16 * (h + 1)]))
+                for m in range(4):
+                    mm1(o, h, m, xg[:])
 
-        for h in range(2):
-            wb = tile([P, PACK * HALF], BF16, "wb%d" % h)
-            cv = CAST_V[h]
-            if cv < HALF:
-                cast(nc.scalar.copy, wb[:, PACK * cv :], wh[h][:, :, cv:])
-            cast(nc.vector.tensor_copy, wb[:, : PACK * cv], wh[h][:, :, :cv])
-            wc = tile([P, HALF], U32, "wc%d" % h)
-            ws = tile([P, HALF], U8, "ws%d" % h)
-            nc.vector.quantize_mx(wc[:].bitcast(FP8X4), ws[:], wb[:])
-            for m in range(2):
-                mm1(1, 2 * h + m, wc[:, m * P : (m + 1) * P], ws[:, m * P : (m + 1) * P])
+        out_t = out.rearrange("(h c e) g -> h e c g", h=2, e=2)
+        ys = {}
+        pair = {}
 
-        z = [tile([P, H], BF16, "z%d" % d) for d in range(D)]
-        out_d = out.rearrange("(v d) g -> d v g", d=D)
-        zqs = {}
-        scs = {}
-        turn_bank = (0, 1, 2, 3)
-        sc_bank = (4, 5, 6, 7)
+        def leave(h, m, eng_copy):
+            ys[h, m] = tile([P, 2, P], F32, "ys%d%d" % (h, m))
+            pair[h, m] = tile([P, P], F32, "pair%d%d" % (h, m))
+            eng_copy(ys[h, m][:], y[h][m][:, 0:HALF].rearrange("p (c e) -> p e c", e=2))
+            yv = ys[h, m][:].rearrange("p e (v a) -> p e v a", a=2)
+            nc.vector.tensor_tensor(
+                pair[h, m][:].rearrange("p (v a) -> p v a", a=2), yv[:, 0, :, ::-1], yv[:, 1, :, ::-1], ADD
+            )
 
-        def turn(d):
-            zt = bank(turn_bank[d], "zt%d" % d)
-            words = z[d][:].bitcast(F32)
+        rest = {}
+
+        def sums(h, e):
+            rest[h, e] = bank(2 * h + e, "rest%d%d" % (h, e))
+            for m in range(4):
+                cols = rest[h, e][:, m * P : (m + 1) * P]
+                nc.tensor.matmul(cols, ys[h, m][:, 1 - e, :], ident[:], is_transpose=True, start=True, stop=False)
+                nc.tensor.matmul(cols, pair[h, m][:], ident[:], is_transpose=True, start=False, stop=True)
+
+        zq = {}
+
+        zs_rows = {}
+
+        def scale(h, e):
+            z = tile([P, H], BF16, "z%d%d" % (h, e))
+            zs_rows[h, e] = z
+            dst = z[:].rearrange("c (u p s) -> c u p s", u=2, s=2)
+            src = rest[h, e][:].rearrange("c (p u s) -> c u p s", u=2, s=2)
+            if (h, e) == (1, 1):
+                nc.vector.tensor_scalar(dst, src, nrm[:, h, e : e + 1], None, MULT)
+            else:
+                nc.scalar.activation(dst, src, COPY, scale=nrm[:, h, e : e + 1])
+
+        def turn(h, e):
+            zt = bank(4 + 2 * h + e, "zt%d%d" % (h, e))
+            words = zs_rows[h, e][:].bitcast(F32)
             for u in range(2):
                 nc.tensor.transpose(zt[:, u * P : (u + 1) * P], words[:, u * P : (u + 1) * P], ident[:])
-            zq = tile([P, V * PACK], BF16, "zq%d" % d)
+            zq[h, e] = tile([P, P * PACK], BF16, "zq%d%d" % (h, e))
             nc.scalar.copy(
-                zq[:].bitcast(F32).rearrange("p (v u) -> p v u", u=2), zt[:, 0:256].rearrange("p (u v) -> p v u", u=2)
+                zq[h, e][:].bitcast(F32).rearrange("p (c u) -> p c u", u=2),
+                zt[:, 0:256].rearrange("p (u c) -> p c u", u=2),
             )
-            zqs[d] = zq
 
-        def score(d):
-            zq = zqs[d]
-            zc = tile([P, V], U32, "zc%d" % d)
-            zs = tile([P, V], U8, "zs%d" % d)
-            nc.vector.quantize_mx(zc[:].bitcast(FP8X4), zs[:], zq[:])
-            sc = bank(sc_bank[d], "sc%d" % d)
+        scs = {}
+        ress = {}
+
+        def score(h, e):
+            zc = tile([P, P], U32, "zc%d%d" % (h, e))
+            zs = tile([P, P], U8, "zs%d%d" % (h, e))
+            nc.vector.quantize_mx(zc[:].bitcast(FP8X4), zs[:], zq[h, e][:])
+            sc = bank(2 * h + e, "sc%d%d" % (h, e))
             nc.tensor.matmul_mx(
                 out=sc[:], lhsT=zc[:].bitcast(FP8X4), lhsT_scale=zs[:], rhs=vg[:].bitcast(FP8X4), rhs_scale=vs_p[:],
                 start=True, stop=True,
             )
-            scs[d] = sc
+            scs[h, e] = sc
 
-        def finish(d):
-            sc = scs[d]
-            res = tile([P, R], F32, "res%d" % d)
-            nc.vector.tensor_tensor(res[:], sc[:], bias_bc[:], ADD)
-            nc.sync.dma_start(out_d[d], res[:])
+        def finish(h, e):
+            res = tile([P, R], F32, "res%d%d" % (h, e))
+            nc.vector.tensor_tensor(res[:], scs[h, e][:], bias_bc[:], ADD)
+            nc.sync.dma_start(out_t[h, e], res[:])
+            ress[h, e] = res
 
-        rest = [bank(4 + d, "rest%d" % d) for d in range(D)]
-        for m in range(4):
-            ys = tile([P, D, V], F32, "ys%d" % m)
-            pair = tile([P, 2, V], F32, "pair%d" % m)
-            if m == 3:
-                nc.vector.tensor_reduce(
-                    pair[:], y[m][:].rearrange("p (v a e) -> p a v e", a=2, e=2), mybir.AxisListType.X, ADD
-                )
-            nc.scalar.copy(ys[:], y[m][:].rearrange("p (v d) -> p d v", d=D))
-            if m < 3:
-                nc.vector.tensor_tensor(pair[:], ys[:, 0:D:2, :], ys[:, 1:D:2, :], ADD)
-            for d in range(D):
-                cols = rest[d][:, m * P : (m + 1) * P]
-                nc.tensor.matmul(cols, pair[:, 1 - d // 2, :], ident[:], is_transpose=True, start=True, stop=False)
-                nc.tensor.matmul(cols, ys[:, d ^ 1, :], ident[:], is_transpose=True, start=False, stop=True)
-        for d in range(D):
-            dst = z[d][:].rearrange("v (u p e) -> v u p e", u=2, e=2)
-            src = rest[d][:].rearrange("v (p u e) -> v u p e", u=2, e=2)
-            if d % 2 == 0:
-                nc.scalar.activation(dst, src, COPY, scale=nrm[:, d : d + 1])
-            else:
-                nc.vector.tensor_scalar(dst, src, nrm[:, d : d + 1], None, MULT)
-        for d in range(D):
-            turn(d)
-        vg = tile([P, R], U32, "vg", tag="pair1")
+        for h in range(2):
+            for m in range(4):
+                leave(h, m, nc.vector.tensor_copy if m == 3 else nc.scalar.copy)
+        vg = tile([P, R], U32, "vg")
         nc.vector.tensor_copy(vg[:], vw[:].indirect(items_sb[:]))
-        for d in range(D):
-            score(d)
-        for d in range(D):
-            finish(d)
+        order = [(h, e) for h in range(2) for e in range(2)]
+        for stage in (sums, scale, turn, score, finish):
+            for h, e in order:
+                stage(h, e)

@@ -45,7 +45,8 @@ def tile_picked_yfism_lin_p_kernel(
         nc.vector.memset(bias_sb[0 : P - 1, :], 0.0)
         xs_p = tile([P, S], U8, "xs_p")
         nc.gpsimd.memset(xs_p[:].bitcast(I32), 0)
-        nc.gpsimd.memset(vs[0 : P - 16, :].bitcast(I32), 0)
+        nc.gpsimd.memset(vs[0:48, :].bitcast(I32), 0)
+        nc.gpsimd.memset(vs[64:P, :].bitcast(I32), 0)
         vs_p = tile([P, R], U8, "vs_p")
         nc.gpsimd.memset(vs_p[:].bitcast(I32), 0)
         ident = tile([P, P], F32, "ident")
@@ -53,14 +54,12 @@ def tile_picked_yfism_lin_p_kernel(
 
         nc.sync.dma_start(offs_sb[:], offs)
         nc.scalar.dma_start(xs[P - 32 : P, :].bitcast(I32), x_scales.rearrange("o q n -> (o q) n").bitcast(I32))
-        nc.sync.dma_start(items_sb[:], items)
-        nc.scalar.dma_start(vs[P - 16 : P, :].bitcast(I32), v_scales[0].bitcast(I32))
+        nc.scalar.dma_start(vs[48:64, :].bitcast(I32), v_scales[0].bitcast(I32))
         nc.scalar.dma_start(bias_sb[P - 1 : P, :], bias[0:1, :])
-        nrm = tile([P, 2, 2], F32, "nrm")
-        nc.scalar.dma_start(nrm[:], norm[0, :].rearrange("(h c e) -> c h e", h=2, e=2))
         wf = [tile([P, PACK * H], F32, "wf%d" % o) for o in range(2)]
-        for o in range(2):
-            nc.sync.dma_start(wf[o][:], w1[512 * o : 512 * (o + 1), :].rearrange("(p j) c -> p (j c)", j=PACK))
+        nc.sync.dma_start(items_sb[:], items)
+        nc.sync.dma_start(wf[0][:], w1[0:512, :].rearrange("(p j) c -> p (j c)", j=PACK))
+        nc.sync.dma_start(wf[1][:], w1[512:1024, :].rearrange("(p j) c -> p (j c)", j=PACK))
 
         xs_g = tile([P, S], U8, "xs_g")
         nc.vector.tensor_copy(xs_g[:], xs[:].indirect(offs_sb[:]))
@@ -86,7 +85,7 @@ def tile_picked_yfism_lin_p_kernel(
         xw.append(load_words("xw1", "vs", x_words[1]))
         vw = load_words("vw", "bias_sb", v_words[0])
         for q in range(4):
-            place(vs_p, 32 * q, vs_g, P - 16 + 4 * q)
+            place(vs_p, 32 * q, vs_g, 48 + 4 * q)
 
         def cast(eng_copy, dst, src):
             eng_copy(dst.rearrange("p (c i t) -> p c t i", i=4, t=PACK), src.rearrange("p t (c i) -> p c t i", i=4))
@@ -137,6 +136,8 @@ def tile_picked_yfism_lin_p_kernel(
                 for m in range(4):
                     mm1(o, h, m, xg[:])
 
+        nrm = tile([P, 2, 2], F32, "nrm", tag="xs")
+        nc.scalar.dma_start(nrm[:], norm[0, :].rearrange("(h c e) -> c h e", h=2, e=2))
         out_t = out.rearrange("(h c e) g -> h e c g", h=2, e=2)
         ys = {}
         pair = {}
@@ -206,7 +207,7 @@ def tile_picked_yfism_lin_p_kernel(
 
         for h in range(2):
             for m in range(4):
-                leave(h, m, nc.vector.tensor_copy if m == 3 else nc.scalar.copy)
+                leave(h, m, nc.vector.tensor_copy if m == 2 else nc.scalar.copy)
         vg = tile([P, R], U32, "vg")
         nc.vector.tensor_copy(vg[:], vw[:].indirect(items_sb[:]))
         order = [(h, e) for h in range(2) for e in range(2)]

@@ -20,6 +20,7 @@ ADD = mybir.AluOpType.add
 P = 128
 PACK = 4
 HALF = S // 2
+WHOLE = 2
 
 
 def tile_picked_yfism_lin_p_kernel(
@@ -43,8 +44,9 @@ def tile_picked_yfism_lin_p_kernel(
         bias_sb = tile([P, G], F32, "bias_sb")
         nc.gpsimd.memset(xs[0 : P - 32, :].bitcast(I32), 0)
         nc.vector.memset(bias_sb[0 : P - 1, :], 0.0)
-        xs_p = tile([P, S], U8, "xs_p")
-        nc.gpsimd.memset(xs_p[:].bitcast(I32), 0)
+        xs_p = [tile([P, S], U8, "xs_p%d" % o) for o in range(2)]
+        for o in range(2):
+            nc.gpsimd.memset(xs_p[o][:].bitcast(I32), 0)
         nc.gpsimd.memset(vs[0:48, :].bitcast(I32), 0)
         nc.gpsimd.memset(vs[64:P, :].bitcast(I32), 0)
         vs_p = tile([P, R], U8, "vs_p")
@@ -76,13 +78,11 @@ def tile_picked_yfism_lin_p_kernel(
             nc.sync.dma_start(window[:].bitcast(I32), words.rearrange("p n t -> p (n t)").bitcast(I32))
             return window
 
-        moves = [(32 * q + 4 * o, P - 32 + 16 * o + 4 * q) for o in range(2) for q in range(4)]
-        for first, row in moves[:4]:
-            place(xs_p, first, xs_g, row)
-        xw = [load_words("xw0", "xs", x_words[0])]
-        for first, row in moves[4:]:
-            place(xs_p, first, xs_g, row)
-        xw.append(load_words("xw1", "vs", x_words[1]))
+        for q in range(4):
+            place(xs_p[0], 32 * q, xs_g, P - 32 + 4 * q)
+        xw = [load_words("xw0", "xs", x_words[0]), load_words("xw1", "vs", x_words[1])]
+        for q in range(4):
+            place(xs_p[1], 32 * q, xs_g, P - 16 + 4 * q)
         vw = load_words("vw", "bias_sb", v_words[0])
         for q in range(4):
             place(vs_p, 32 * q, vs_g, 48 + 4 * q)
@@ -124,7 +124,7 @@ def tile_picked_yfism_lin_p_kernel(
                 lhsT=wc[o][:, m * P : (m + 1) * P].bitcast(FP8X4),
                 lhsT_scale=ws[o][:, m * P : (m + 1) * P],
                 rhs=xg.bitcast(FP8X4),
-                rhs_scale=xs_p[4 * o : P, h * HALF : (h + 1) * HALF],
+                rhs_scale=xs_p[o][:, h * HALF : (h + 1) * HALF],
                 start=(o == 0),
                 stop=(o == 1),
             )
@@ -142,23 +142,37 @@ def tile_picked_yfism_lin_p_kernel(
         ys = {}
         pair = {}
 
-        def leave(h, m, eng_copy):
+        def leave(h, m):
             ys[h, m] = tile([P, 2, P], F32, "ys%d%d" % (h, m))
             pair[h, m] = tile([P, P], F32, "pair%d%d" % (h, m))
-            eng_copy(ys[h, m][:], y[h][m][:, 0:HALF].rearrange("p (c e) -> p e c", e=2))
+            src = y[h][m][:, 0:HALF]
+            pv = pair[h, m][:].rearrange("p (v a) -> p v a", a=2)
             yv = ys[h, m][:].rearrange("p e (v a) -> p e v a", a=2)
-            nc.vector.tensor_tensor(
-                pair[h, m][:].rearrange("p (v a) -> p v a", a=2), yv[:, 0, :, ::-1], yv[:, 1, :, ::-1], ADD
-            )
+            if m == WHOLE:
+                nc.vector.tensor_reduce(pair[h, m][:], src.rearrange("p (c e) -> p c e", e=2), mybir.AxisListType.X, ADD)
+                nc.vector.tensor_tensor(
+                    yv,
+                    src.rearrange("p (v a e) -> p e v a", a=2, e=2),
+                    pv[:, :, ::-1].unsqueeze(1).to_broadcast([P, 2, P // 2, 2]),
+                    ADD,
+                )
+            else:
+                nc.scalar.copy(ys[h, m][:], src.rearrange("p (c e) -> p e c", e=2))
+                nc.vector.tensor_tensor(pv, yv[:, 0, :, ::-1], yv[:, 1, :, ::-1], ADD)
 
         rest = {}
 
-        def sums(h, e):
-            rest[h, e] = bank(2 * h + e, "rest%d%d" % (h, e))
+        def sums(h):
+            for e in range(2):
+                rest[h, e] = bank(2 * h + e, "rest%d%d" % (h, e))
             for m in range(4):
-                cols = rest[h, e][:, m * P : (m + 1) * P]
-                nc.tensor.matmul(cols, ys[h, m][:, 1 - e, :], ident[:], is_transpose=True, start=True, stop=False)
-                nc.tensor.matmul(cols, pair[h, m][:], ident[:], is_transpose=True, start=False, stop=True)
+                for e in range(2):
+                    cols = rest[h, e][:, m * P : (m + 1) * P]
+                    if m == WHOLE:
+                        nc.tensor.transpose(cols, ys[h, m][:, 1 - e, :], ident[:])
+                    else:
+                        nc.tensor.matmul(cols, ys[h, m][:, 1 - e, :], ident[:], is_transpose=True, start=True, stop=False)
+                        nc.tensor.matmul(cols, pair[h, m][:], ident[:], is_transpose=True, start=False, stop=True)
 
         zq = {}
 
@@ -207,10 +221,12 @@ def tile_picked_yfism_lin_p_kernel(
 
         for h in range(2):
             for m in range(4):
-                leave(h, m, nc.vector.tensor_copy if m == 2 else nc.scalar.copy)
+                leave(h, m)
         vg = tile([P, R], U32, "vg")
         nc.vector.tensor_copy(vg[:], vw[:].indirect(items_sb[:]))
         order = [(h, e) for h in range(2) for e in range(2)]
-        for stage in (sums, scale, turn, score, finish):
+        for h in range(2):
+            sums(h)
+        for stage in (scale, turn, score, finish):
             for h, e in order:
                 stage(h, e)

@@ -3,7 +3,7 @@ from contextlib import ExitStack
 import concourse.mybir as mybir
 from concourse.masks import make_identity
 
-K, T, S, D, H, G, R = 1024, 2048, 512, 4, 512, 2048, 512
+K, T, S, H, G, R = 1024, 2048, 512, 512, 2048, 512
 FLOPS = 2 * K * H * S + 2 * H * S * R
 
 F32 = mybir.dt.float32
@@ -19,8 +19,16 @@ ADD = mybir.AluOpType.add
 
 P = 128
 PACK = 4
+PASS = P * PACK
+BANK = 512
+QUAD = 32
+BLOCKS = PASS // 32
 HALF = S // 2
-WHOLE = 2
+CH_TILES = H // P
+X_ROWS = P - 2 * BLOCKS
+V_ROWS = 2 * QUAD - BLOCKS
+VECTOR_TILE = 2
+VECTOR_NORM = (1, 1)
 
 
 def tile_picked_yfism_lin_p_kernel(
@@ -32,201 +40,201 @@ def tile_picked_yfism_lin_p_kernel(
         ps = ctx.enter_context(tc.psum_pool(name="ps", bufs=1))
 
         def bank(b, name):
-            return ps.tile([P, 512], F32, name=name, tag="bank%d" % b)
+            return ps.tile([P, BANK], F32, name=name, tag="bank%d" % b)
 
         def tile(shape, dtype, name, tag=None):
             return sb.tile(shape, dtype, name=name, tag=tag or name, align_bytes=64)
 
         offs_sb = tile([P, S // 16], U16, "offs_sb")
         items_sb = tile([P, R // 16], U16, "items_sb")
-        xs = tile([P, T], U8, "xs")
-        vs = tile([P, G], U8, "vs")
-        bias_sb = tile([P, G], F32, "bias_sb")
-        nc.gpsimd.memset(xs[0 : P - 32, :].bitcast(I32), 0)
-        nc.vector.memset(bias_sb[0 : P - 1, :], 0.0)
-        xs_p = [tile([P, S], U8, "xs_p%d" % o) for o in range(2)]
-        for o in range(2):
-            nc.gpsimd.memset(xs_p[o][:].bitcast(I32), 0)
-        nc.gpsimd.memset(vs[0:48, :].bitcast(I32), 0)
-        nc.gpsimd.memset(vs[64:P, :].bitcast(I32), 0)
-        vs_p = tile([P, R], U8, "vs_p")
-        nc.gpsimd.memset(vs_p[:].bitcast(I32), 0)
+        x_scale_win = tile([P, T], U8, "x_scale_win")
+        v_scale_win = tile([P, G], U8, "v_scale_win")
+        bias_win = tile([P, G], F32, "bias_win")
+        nc.gpsimd.memset(x_scale_win[0:X_ROWS, :].bitcast(I32), 0)
+        nc.vector.memset(bias_win[0 : P - 1, :], 0.0)
+        x_plane = tile([P, S], U8, "x_plane")
+        nc.gpsimd.memset(x_plane[:].bitcast(I32), 0)
+        nc.gpsimd.memset(v_scale_win[0:V_ROWS, :].bitcast(I32), 0)
+        nc.gpsimd.memset(v_scale_win[V_ROWS + BLOCKS : P, :].bitcast(I32), 0)
+        v_plane = tile([P, R], U8, "v_plane")
+        nc.gpsimd.memset(v_plane[:].bitcast(I32), 0)
         ident = tile([P, P], F32, "ident")
         make_identity(nc, ident[:])
 
         nc.sync.dma_start(offs_sb[:], offs)
-        nc.scalar.dma_start(xs[P - 32 : P, :].bitcast(I32), x_scales.rearrange("o q n -> (o q) n").bitcast(I32))
-        nc.scalar.dma_start(vs[48:64, :].bitcast(I32), v_scales[0].bitcast(I32))
-        nc.scalar.dma_start(bias_sb[P - 1 : P, :], bias[0:1, :])
-        wf = [tile([P, PACK * H], F32, "wf%d" % o) for o in range(2)]
+        nc.scalar.dma_start(x_scale_win[X_ROWS:P, :].bitcast(I32), x_scales.rearrange("o q n -> (o q) n").bitcast(I32))
+        nc.scalar.dma_start(v_scale_win[V_ROWS : V_ROWS + BLOCKS, :].bitcast(I32), v_scales[0].bitcast(I32))
+        nc.scalar.dma_start(bias_win[P - 1 : P, :], bias[0:1, :])
+        w_raw = [tile([P, PACK * H], F32, "w_raw%d" % o) for o in range(2)]
         nc.sync.dma_start(items_sb[:], items)
-        nc.sync.dma_start(wf[0][:], w1[0:512, :].rearrange("(p j) c -> p (j c)", j=PACK))
-        nc.sync.dma_start(wf[1][:], w1[512:1024, :].rearrange("(p j) c -> p (j c)", j=PACK))
+        for o in range(2):
+            nc.sync.dma_start(w_raw[o][:], w1[o * PASS : (o + 1) * PASS, :].rearrange("(p j) c -> p (j c)", j=PACK))
 
-        xs_g = tile([P, S], U8, "xs_g")
-        nc.vector.tensor_copy(xs_g[:], xs[:].indirect(offs_sb[:]))
-        vs_g = tile([P, R], U8, "vs_g")
-        nc.vector.tensor_copy(vs_g[:], vs[:].indirect(items_sb[:]))
-        bias_g = tile([P, R], F32, "bias_g")
-        nc.vector.tensor_copy(bias_g[:], bias_sb[:].indirect(items_sb[:]))
+        x_scale_picked = tile([P, S], U8, "x_scale_picked")
+        nc.vector.tensor_copy(x_scale_picked[:], x_scale_win[:].indirect(offs_sb[:]))
+        v_scale_picked = tile([P, R], U8, "v_scale_picked")
+        nc.vector.tensor_copy(v_scale_picked[:], v_scale_win[:].indirect(items_sb[:]))
+        bias_picked = tile([P, R], F32, "bias_picked")
+        nc.vector.tensor_copy(bias_picked[:], bias_win[:].indirect(items_sb[:]))
 
-        def place(plane, first, gathered, row):
-            nc.sync.dma_start(plane[first : first + 4, :].bitcast(I32), gathered[row : row + 4, :].bitcast(I32))
+        def place_scales(plane, a, picked, first_row):
+            for q in range(P // QUAD):
+                rows = picked[first_row + 4 * q : first_row + 4 * q + 4, :]
+                nc.sync.dma_start(plane[QUAD * q + a : QUAD * q + a + 4, :].bitcast(I32), rows.bitcast(I32))
 
         def load_words(name, tag, words):
             window = tile([P, T], U32, name, tag=tag)
             nc.sync.dma_start(window[:].bitcast(I32), words.rearrange("p n t -> p (n t)").bitcast(I32))
             return window
 
-        for q in range(4):
-            place(xs_p[0], 32 * q, xs_g, P - 32 + 4 * q)
-        xw = [load_words("xw0", "xs", x_words[0]), load_words("xw1", "vs", x_words[1])]
-        for q in range(4):
-            place(xs_p[1], 32 * q, xs_g, P - 16 + 4 * q)
-        vw = load_words("vw", "bias_sb", v_words[0])
-        for q in range(4):
-            place(vs_p, 32 * q, vs_g, 48 + 4 * q)
+        x_win = []
+        for o, tag in enumerate(("x_scale_win", "v_scale_win")):
+            place_scales(x_plane, 4 * o, x_scale_picked, X_ROWS + BLOCKS * o)
+            x_win.append(load_words("x_win%d" % o, tag, x_words[o]))
+        v_win = load_words("v_win", "bias_win", v_words[0])
+        place_scales(v_plane, 0, v_scale_picked, V_ROWS)
 
-        def cast(eng_copy, dst, src):
-            eng_copy(dst.rearrange("p (c i t) -> p c t i", i=4, t=PACK), src.rearrange("p t (c i) -> p c t i", i=4))
+        bias_turned = bank(7, "bias_turned")
+        for c in range(R // P):
+            nc.tensor.transpose(bias_turned[:, c * P : (c + 1) * P], bias_picked[:, c * P : (c + 1) * P], ident[:])
 
-        bt = bank(7, "bt")
-        for c in range(4):
-            nc.tensor.transpose(bt[:, c * P : (c + 1) * P], bias_g[:, c * P : (c + 1) * P], ident[:])
+        w_codes = [tile([P, H], U32, "w_codes%d" % o) for o in range(2)]
+        w_scales = [tile([P, H], U8, "w_scales%d" % o) for o in range(2)]
 
-        wc = [tile([P, H], U32, "wc%d" % o) for o in range(2)]
-        ws = [tile([P, H], U8, "ws%d" % o) for o in range(2)]
+        def quantise_w(o, copies):
+            w_bf = tile([P, PACK * H], BF16, "w_bf%d" % o)
+            rows = w_raw[o][:].rearrange("p (j c) -> p j c", j=PACK)
+            cols = H // 2
+            for n in range(2):
+                dst = w_bf[:, n * PACK * cols : (n + 1) * PACK * cols]
+                src = rows[:, :, n * cols : (n + 1) * cols]
+                copies[n](
+                    dst.rearrange("p (c i t) -> p c t i", i=4, t=PACK), src.rearrange("p t (c i) -> p c t i", i=4)
+                )
+            nc.vector.quantize_mx(w_codes[o][:].bitcast(FP8X4), w_scales[o][:], w_bf[:])
 
-        def quant_w(o, casts):
-            wb = tile([P, PACK * H], BF16, "wb%d" % o)
-            wv = wf[o][:].rearrange("p (j c) -> p j c", j=PACK)
-            for h in range(2):
-                cast(casts[h], wb[:, h * 1024 : (h + 1) * 1024], wv[:, :, h * 256 : (h + 1) * 256])
-            nc.vector.quantize_mx(wc[o][:].bitcast(FP8X4), ws[o][:], wb[:])
+        quantise_w(0, (nc.scalar.copy, nc.scalar.copy))
 
-        quant_w(0, (nc.scalar.copy, nc.scalar.copy))
-
-        bias_col = tile([P, 4], F32, "bias_col", tag="wf0")
-        nc.scalar.copy(bias_col[:], bt[:, P - 1 : 512 : P])
-        bb = bank(6, "bb")
-        for c in range(4):
-            nc.tensor.transpose(bb[:, c * P : (c + 1) * P], bias_col[:, c : c + 1].to_broadcast([P, P]), ident[:])
-        bias_bc = tile([P, R], F32, "bias_bc")
-
-        quant_w(1, (nc.scalar.copy, nc.vector.tensor_copy))
-        nc.scalar.copy(bias_bc[:], bb[:])
-
-        y = [[bank(4 * h + m, "y%d%d" % (h, m)) for m in range(4)] for h in range(2)]
-
-        def mm1(o, h, m, xg):
-            nc.tensor.matmul_mx(
-                out=y[h][m][:, 0:HALF],
-                lhsT=wc[o][:, m * P : (m + 1) * P].bitcast(FP8X4),
-                lhsT_scale=ws[o][:, m * P : (m + 1) * P],
-                rhs=xg.bitcast(FP8X4),
-                rhs_scale=xs_p[o][:, h * HALF : (h + 1) * HALF],
-                start=(o == 0),
-                stop=(o == 1),
+        bias_col = tile([P, R // P], F32, "bias_col", tag="w_raw0")
+        nc.scalar.copy(bias_col[:], bias_turned[:, P - 1 : BANK : P])
+        bias_spread = bank(6, "bias_spread")
+        for c in range(R // P):
+            nc.tensor.transpose(
+                bias_spread[:, c * P : (c + 1) * P], bias_col[:, c : c + 1].to_broadcast([P, P]), ident[:]
             )
+        bias_all = tile([P, R], F32, "bias_all")
 
+        quantise_w(1, (nc.scalar.copy, nc.vector.tensor_copy))
+        nc.scalar.copy(bias_all[:], bias_spread[:])
+
+        y = [[bank(CH_TILES * h + m, "y%d%d" % (h, m)) for m in range(CH_TILES)] for h in range(2)]
+        list_cols = HALF // 16
         for o in range(2):
             for h in range(2):
-                xg = tile([P, HALF], U32, "xg%d%d" % (o, h))
-                nc.vector.tensor_copy(xg[:], xw[o][:].indirect(offs_sb[:, 16 * h : 16 * (h + 1)]))
-                for m in range(4):
-                    mm1(o, h, m, xg[:])
+                x_picked = tile([P, HALF], U32, "x_picked%d%d" % (o, h))
+                nc.vector.tensor_copy(x_picked[:], x_win[o][:].indirect(offs_sb[:, list_cols * h : list_cols * (h + 1)]))
+                for m in range(CH_TILES):
+                    nc.tensor.matmul_mx(
+                        out=y[h][m][:, 0:HALF],
+                        lhsT=w_codes[o][:, m * P : (m + 1) * P].bitcast(FP8X4),
+                        lhsT_scale=w_scales[o][:, m * P : (m + 1) * P],
+                        rhs=x_picked[:].bitcast(FP8X4),
+                        rhs_scale=x_plane[4 * o : P, h * HALF : (h + 1) * HALF],
+                        start=(o == 0),
+                        stop=(o == 1),
+                    )
 
-        nrm = tile([P, 2, 2], F32, "nrm", tag="xs")
-        nc.scalar.dma_start(nrm[:], norm[0, :].rearrange("(h c e) -> c h e", h=2, e=2))
-        out_t = out.rearrange("(h c e) g -> h e c g", h=2, e=2)
-        ys = {}
+        norm_col = tile([P, 2, 2], F32, "norm_col", tag="x_scale_win")
+        nc.scalar.dma_start(norm_col[:], norm[0, :].rearrange("(h c e) -> c h e", h=2, e=2))
+        out_tiles = out.rearrange("(h c e) g -> h e c g", h=2, e=2)
+        by_parity = {}
         pair = {}
 
-        def leave(h, m):
-            ys[h, m] = tile([P, 2, P], F32, "ys%d%d" % (h, m))
+        def empty_y(h, m):
+            by_parity[h, m] = tile([P, 2, P], F32, "by_parity%d%d" % (h, m))
             pair[h, m] = tile([P, P], F32, "pair%d%d" % (h, m))
             src = y[h][m][:, 0:HALF]
-            pv = pair[h, m][:].rearrange("p (v a) -> p v a", a=2)
-            yv = ys[h, m][:].rearrange("p e (v a) -> p e v a", a=2)
-            if m == WHOLE:
+            pair_va = pair[h, m][:].rearrange("p (v a) -> p v a", a=2)
+            parity_va = by_parity[h, m][:].rearrange("p e (v a) -> p e v a", a=2)
+            if m == VECTOR_TILE:
                 nc.vector.tensor_reduce(pair[h, m][:], src.rearrange("p (c e) -> p c e", e=2), mybir.AxisListType.X, ADD)
                 nc.vector.tensor_tensor(
-                    yv,
+                    parity_va,
                     src.rearrange("p (v a e) -> p e v a", a=2, e=2),
-                    pv[:, :, ::-1].unsqueeze(1).to_broadcast([P, 2, P // 2, 2]),
+                    pair_va[:, :, ::-1].unsqueeze(1).to_broadcast([P, 2, P // 2, 2]),
                     ADD,
                 )
             else:
-                nc.scalar.copy(ys[h, m][:], src.rearrange("p (c e) -> p e c", e=2))
-                nc.vector.tensor_tensor(pv, yv[:, 0, :, ::-1], yv[:, 1, :, ::-1], ADD)
+                nc.scalar.copy(by_parity[h, m][:], src.rearrange("p (c e) -> p e c", e=2))
+                nc.vector.tensor_tensor(pair_va, parity_va[:, 0, :, ::-1], parity_va[:, 1, :, ::-1], ADD)
 
-        rest = {}
+        others = {}
 
-        def sums(h):
+        def sum_others(h):
             for e in range(2):
-                rest[h, e] = bank(2 * h + e, "rest%d%d" % (h, e))
-            for m in range(4):
+                others[h, e] = bank(2 * h + e, "others%d%d" % (h, e))
+            for m in range(CH_TILES):
                 for e in range(2):
-                    cols = rest[h, e][:, m * P : (m + 1) * P]
-                    if m == WHOLE:
-                        nc.tensor.transpose(cols, ys[h, m][:, 1 - e, :], ident[:])
+                    cols = others[h, e][:, m * P : (m + 1) * P]
+                    opposite = by_parity[h, m][:, 1 - e, :]
+                    if m == VECTOR_TILE:
+                        nc.tensor.transpose(cols, opposite, ident[:])
                     else:
-                        nc.tensor.matmul(cols, ys[h, m][:, 1 - e, :], ident[:], is_transpose=True, start=True, stop=False)
+                        nc.tensor.matmul(cols, opposite, ident[:], is_transpose=True, start=True, stop=False)
                         nc.tensor.matmul(cols, pair[h, m][:], ident[:], is_transpose=True, start=False, stop=True)
 
-        zq = {}
+        z_rows = {}
+        z_cols = {}
+        scores = {}
 
-        zs_rows = {}
-
-        def scale(h, e):
-            z = tile([P, H], BF16, "z%d%d" % (h, e))
-            zs_rows[h, e] = z
-            dst = z[:].rearrange("c (u p s) -> c u p s", u=2, s=2)
-            src = rest[h, e][:].rearrange("c (p u s) -> c u p s", u=2, s=2)
-            if (h, e) == (1, 1):
-                nc.vector.tensor_scalar(dst, src, nrm[:, h, e : e + 1], None, MULT)
+        def apply_norm(h, e):
+            z_rows[h, e] = tile([P, H], BF16, "z_rows%d%d" % (h, e))
+            dst = z_rows[h, e][:].rearrange("c (u p s) -> c u p s", u=2, s=2)
+            src = others[h, e][:].rearrange("c (p u s) -> c u p s", u=2, s=2)
+            if (h, e) == VECTOR_NORM:
+                nc.vector.tensor_scalar(dst, src, norm_col[:, h, e : e + 1], None, MULT)
             else:
-                nc.scalar.activation(dst, src, COPY, scale=nrm[:, h, e : e + 1])
+                nc.scalar.activation(dst, src, COPY, scale=norm_col[:, h, e : e + 1])
 
         def turn(h, e):
-            zt = bank(4 + 2 * h + e, "zt%d%d" % (h, e))
-            words = zs_rows[h, e][:].bitcast(F32)
+            turned = bank(CH_TILES + 2 * h + e, "turned%d%d" % (h, e))
+            pairs = z_rows[h, e][:].bitcast(F32)
             for u in range(2):
-                nc.tensor.transpose(zt[:, u * P : (u + 1) * P], words[:, u * P : (u + 1) * P], ident[:])
-            zq[h, e] = tile([P, P * PACK], BF16, "zq%d%d" % (h, e))
+                nc.tensor.transpose(turned[:, u * P : (u + 1) * P], pairs[:, u * P : (u + 1) * P], ident[:])
+            z_cols[h, e] = tile([P, P * PACK], BF16, "z_cols%d%d" % (h, e))
             nc.scalar.copy(
-                zq[h, e][:].bitcast(F32).rearrange("p (c u) -> p c u", u=2),
-                zt[:, 0:256].rearrange("p (u c) -> p c u", u=2),
+                z_cols[h, e][:].bitcast(F32).rearrange("p (c u) -> p c u", u=2),
+                turned[:, 0 : 2 * P].rearrange("p (u c) -> p c u", u=2),
             )
-
-        scs = {}
-        ress = {}
 
         def score(h, e):
-            zc = tile([P, P], U32, "zc%d%d" % (h, e))
-            zs = tile([P, P], U8, "zs%d%d" % (h, e))
-            nc.vector.quantize_mx(zc[:].bitcast(FP8X4), zs[:], zq[h, e][:])
-            sc = bank(2 * h + e, "sc%d%d" % (h, e))
+            z_codes = tile([P, P], U32, "z_codes%d%d" % (h, e))
+            z_scales = tile([P, P], U8, "z_scales%d%d" % (h, e))
+            nc.vector.quantize_mx(z_codes[:].bitcast(FP8X4), z_scales[:], z_cols[h, e][:])
+            scores[h, e] = bank(2 * h + e, "scores%d%d" % (h, e))
             nc.tensor.matmul_mx(
-                out=sc[:], lhsT=zc[:].bitcast(FP8X4), lhsT_scale=zs[:], rhs=vg[:].bitcast(FP8X4), rhs_scale=vs_p[:],
-                start=True, stop=True,
+                out=scores[h, e][:],
+                lhsT=z_codes[:].bitcast(FP8X4),
+                lhsT_scale=z_scales[:],
+                rhs=v_picked[:].bitcast(FP8X4),
+                rhs_scale=v_plane[:],
+                start=True,
+                stop=True,
             )
-            scs[h, e] = sc
 
-        def finish(h, e):
-            res = tile([P, R], F32, "res%d%d" % (h, e))
-            nc.vector.tensor_tensor(res[:], scs[h, e][:], bias_bc[:], ADD)
-            nc.sync.dma_start(out_t[h, e], res[:])
-            ress[h, e] = res
+        def store(h, e):
+            result = tile([P, R], F32, "result%d%d" % (h, e))
+            nc.vector.tensor_tensor(result[:], scores[h, e][:], bias_all[:], ADD)
+            nc.sync.dma_start(out_tiles[h, e], result[:])
 
         for h in range(2):
-            for m in range(4):
-                leave(h, m)
-        vg = tile([P, R], U32, "vg")
-        nc.vector.tensor_copy(vg[:], vw[:].indirect(items_sb[:]))
-        order = [(h, e) for h in range(2) for e in range(2)]
+            for m in range(CH_TILES):
+                empty_y(h, m)
+        v_picked = tile([P, R], U32, "v_picked")
+        nc.vector.tensor_copy(v_picked[:], v_win[:].indirect(items_sb[:]))
         for h in range(2):
-            sums(h)
-        for stage in (scale, turn, score, finish):
-            for h, e in order:
-                stage(h, e)
+            sum_others(h)
+        for stage in (apply_norm, turn, score, store):
+            for h in range(2):
+                for e in range(2):
+                    stage(h, e)

@@ -173,15 +173,16 @@ def tile_picked_yfism_lin_p_kernel(
         def sum_others(h):
             for e in range(2):
                 others[h, e] = bank(2 * h + e, "others%d%d" % (h, e))
-            for m in range(CH_TILES):
-                for e in range(2):
-                    cols = others[h, e][:, m * P : (m + 1) * P]
-                    opposite = by_parity[h, m][:, 1 - e, :]
-                    if m == VECTOR_TILE:
-                        nc.tensor.transpose(cols, opposite, ident[:])
-                    else:
-                        nc.tensor.matmul(cols, opposite, ident[:], is_transpose=True, start=True, stop=False)
-                        nc.tensor.matmul(cols, pair[h, m][:], ident[:], is_transpose=True, start=False, stop=True)
+            early = [(m, e) for m in range(2) for e in range(2)]
+            late = [(m, e) for e in range(2) for m in range(2, CH_TILES)]
+            for m, e in early + late:
+                cols = others[h, e][:, m * P : (m + 1) * P]
+                opposite = by_parity[h, m][:, 1 - e, :]
+                if m == VECTOR_TILE:
+                    nc.tensor.transpose(cols, opposite, ident[:])
+                else:
+                    nc.tensor.matmul(cols, opposite, ident[:], is_transpose=True, start=True, stop=False)
+                    nc.tensor.matmul(cols, pair[h, m][:], ident[:], is_transpose=True, start=False, stop=True)
 
         z_rows = {}
         z_cols = {}
@@ -207,25 +208,30 @@ def tile_picked_yfism_lin_p_kernel(
                 turned[:, 0 : 2 * P].rearrange("p (u c) -> p c u", u=2),
             )
 
-        def score(h, e):
+        codes = {}
+
+        def quantise_z(h, e):
             z_codes = tile([P, P], U32, "z_codes%d%d" % (h, e))
             z_scales = tile([P, P], U8, "z_scales%d%d" % (h, e))
             nc.vector.quantize_mx(z_codes[:].bitcast(FP8X4), z_scales[:], z_cols[h, e][:])
-            scores[h, e] = bank(2 * h + e, "scores%d%d" % (h, e))
+            codes[h, e] = (z_codes, z_scales)
+
+        def score(h, e, a, b, on_bank):
+            scores[h, e, a] = bank(on_bank, "scores%d%d%d" % (h, e, a))
             nc.tensor.matmul_mx(
-                out=scores[h, e][:],
-                lhsT=z_codes[:].bitcast(FP8X4),
-                lhsT_scale=z_scales[:],
-                rhs=v_picked[:].bitcast(FP8X4),
-                rhs_scale=v_plane[:],
+                out=scores[h, e, a][:, 0 : b - a],
+                lhsT=codes[h, e][0][:].bitcast(FP8X4),
+                lhsT_scale=codes[h, e][1][:],
+                rhs=v_picked[:, a:b].bitcast(FP8X4),
+                rhs_scale=v_plane[:, a:b],
                 start=True,
                 stop=True,
             )
 
-        def store(h, e):
-            result = tile([P, R], F32, "result%d%d" % (h, e))
-            nc.vector.tensor_tensor(result[:], scores[h, e][:], bias_all[:], ADD)
-            nc.sync.dma_start(out_tiles[h, e], result[:])
+        def store(h, e, a, b, first):
+            result = tile([P, b - a], F32, "result%d%d%d" % (h, e, a))
+            nc.vector.tensor_tensor(result[:], scores[h, e, first][:, a - first : b - first], bias_all[:, a:b], ADD)
+            nc.sync.dma_start(out_tiles[h, e, :, a:b], result[:])
 
         for h in range(2):
             for m in range(CH_TILES):
@@ -234,7 +240,19 @@ def tile_picked_yfism_lin_p_kernel(
         nc.vector.tensor_copy(v_picked[:], v_win[:].indirect(items_sb[:]))
         for h in range(2):
             sum_others(h)
-        for stage in (apply_norm, turn, score, store):
-            for h in range(2):
-                for e in range(2):
-                    stage(h, e)
+        tiles = [(h, e) for h in range(2) for e in range(2)]
+        for stage in (apply_norm, turn):
+            for h, e in tiles:
+                stage(h, e)
+        quantise_z(0, 0)
+        score(0, 0, 0, R // 2, 0)
+        score(0, 0, R // 2, R, CH_TILES)
+        for h, e in tiles[1:3]:
+            quantise_z(h, e)
+            score(h, e, 0, R, 2 * h + e)
+        store(0, 0, 0, R // 2, 0)
+        quantise_z(1, 1)
+        score(1, 1, 0, R, 3)
+        store(0, 0, R // 2, R, R // 2)
+        for h, e in tiles[1:]:
+            store(h, e, 0, R, 0)

@@ -3,7 +3,7 @@ from contextlib import ExitStack
 import concourse.mybir as mybir
 from concourse.masks import make_identity
 
-K, T, S, H, G, R = 1024, 2048, 512, 512, 2048, 512
+K, T, S, H, G, R, D = 1024, 2048, 512, 512, 2048, 512, 4
 FLOPS = 2 * K * H * S + 2 * H * S * R
 
 F32 = mybir.dt.float32
@@ -23,12 +23,10 @@ PASS = P * PACK
 BANK = 512
 QUAD = 32
 BLOCKS = PASS // 32
-HALF = S // 2
-CH_TILES = H // P
+HALF = H // 2
 X_ROWS = P - 2 * BLOCKS
 V_ROWS = 2 * QUAD - BLOCKS
-VECTOR_TILE = 2
-VECTOR_NORM = (1, 1)
+SCALAR_COLS = 96
 
 
 def tile_picked_yfism_lin_p_kernel(
@@ -61,17 +59,25 @@ def tile_picked_yfism_lin_p_kernel(
         ident = tile([P, P], F32, "ident")
         make_identity(nc, ident[:])
 
+        def load_words(name, tag, words):
+            window = tile([P, T], U32, name, tag=tag)
+            nc.sync.dma_start(window[:].bitcast(I32), words.rearrange("p n t -> p (n t)").bitcast(I32))
+            return window
+
         nc.sync.dma_start(offs_sb[:], offs)
         nc.scalar.dma_start(x_scale_win[X_ROWS:P, :].bitcast(I32), x_scales.rearrange("o q n -> (o q) n").bitcast(I32))
         nc.scalar.dma_start(v_scale_win[V_ROWS : V_ROWS + BLOCKS, :].bitcast(I32), v_scales[0].bitcast(I32))
         nc.scalar.dma_start(bias_win[P - 1 : P, :], bias[0:1, :])
-        w_raw = [tile([P, PACK * H], F32, "w_raw%d" % o) for o in range(2)]
         nc.sync.dma_start(items_sb[:], items)
-        for o in range(2):
-            nc.sync.dma_start(w_raw[o][:], w1[o * PASS : (o + 1) * PASS, :].rearrange("(p j) c -> p (j c)", j=PACK))
+        w_raw0 = tile([P, PACK, H], F32, "w_raw0")
+        nc.sync.dma_start(w_raw0[:].rearrange("p j c -> p (j c)"), w1[0:PASS, :].rearrange("(p j) c -> p (j c)", j=PACK))
+        x_win = [load_words("x_win0", None, x_words[0])]
+
+        def by_item(picked):
+            return picked[:].rearrange("p (d v) -> p v d", d=D)
 
         x_scale_picked = tile([P, S], U8, "x_scale_picked")
-        nc.vector.tensor_copy(x_scale_picked[:], x_scale_win[:].indirect(offs_sb[:]))
+        nc.vector.tensor_copy(by_item(x_scale_picked), x_scale_win[:].indirect(offs_sb[:]))
         v_scale_picked = tile([P, R], U8, "v_scale_picked")
         nc.vector.tensor_copy(v_scale_picked[:], v_scale_win[:].indirect(items_sb[:]))
         bias_picked = tile([P, R], F32, "bias_picked")
@@ -82,38 +88,36 @@ def tile_picked_yfism_lin_p_kernel(
                 rows = picked[first_row + 4 * q : first_row + 4 * q + 4, :]
                 nc.sync.dma_start(plane[QUAD * q + a : QUAD * q + a + 4, :].bitcast(I32), rows.bitcast(I32))
 
-        def load_words(name, tag, words):
-            window = tile([P, T], U32, name, tag=tag)
-            nc.sync.dma_start(window[:].bitcast(I32), words.rearrange("p n t -> p (n t)").bitcast(I32))
-            return window
-
-        x_win = []
-        for o, tag in enumerate(("x_scale_win", "v_scale_win")):
-            place_scales(x_plane, 4 * o, x_scale_picked, X_ROWS + BLOCKS * o)
-            x_win.append(load_words("x_win%d" % o, tag, x_words[o]))
-        v_win = load_words("v_win", "bias_win", v_words[0])
-        place_scales(v_plane, 0, v_scale_picked, V_ROWS)
+        place_scales(x_plane, 0, x_scale_picked, X_ROWS)
+        x_win.append(load_words("x_win1", "x_scale_win", x_words[1]))
+        place_scales(x_plane, 4, x_scale_picked, X_ROWS + BLOCKS)
+        w_raw1 = []
+        w_raw1.append(tile([P, PACK, HALF], F32, "w_raw10", tag="v_scale_win"))
+        w_raw1.append(tile([P, PACK, HALF], F32, "w_raw11", tag="bias_win"))
+        for h in range(2):
+            nc.sync.dma_start(w_raw1[h][:], w1[PASS:K, h * HALF : (h + 1) * HALF].rearrange("(p j) c -> p j c", j=PACK))
 
         bias_turned = bank(7, "bias_turned")
         for c in range(R // P):
             nc.tensor.transpose(bias_turned[:, c * P : (c + 1) * P], bias_picked[:, c * P : (c + 1) * P], ident[:])
+        v_win = load_words("v_win", "bias_picked", v_words[0])
+        place_scales(v_plane, 0, v_scale_picked, V_ROWS)
+        norm_col = tile([P, D], F32, "norm_col", tag="x_scale_picked")
+        nc.sync.dma_start(norm_col[:], norm[0, :].rearrange("(v d) -> v d", d=D))
 
-        w_codes = [tile([P, H], U32, "w_codes%d" % o) for o in range(2)]
-        w_scales = [tile([P, H], U8, "w_scales%d" % o) for o in range(2)]
+        def round_w(copy, w_bf, raw, a, b):
+            dst = w_bf[:, PACK * a : PACK * b]
+            copy(dst.rearrange("p (c i t) -> p c t i", i=4, t=PACK), raw[:, :, a:b].rearrange("p t (c i) -> p c t i", i=4))
 
-        def quantise_w(o, copies):
-            w_bf = tile([P, PACK * H], BF16, "w_bf%d" % o)
-            rows = w_raw[o][:].rearrange("p (j c) -> p j c", j=PACK)
-            cols = H // 2
-            for n in range(2):
-                dst = w_bf[:, n * PACK * cols : (n + 1) * PACK * cols]
-                src = rows[:, :, n * cols : (n + 1) * cols]
-                copies[n](
-                    dst.rearrange("p (c i t) -> p c t i", i=4, t=PACK), src.rearrange("p t (c i) -> p c t i", i=4)
-                )
-            nc.vector.quantize_mx(w_codes[o][:].bitcast(FP8X4), w_scales[o][:], w_bf[:])
+        def quantise(name, values, cols):
+            codes = tile([P, cols], U32, name + "_codes")
+            scales = tile([P, cols], U8, name + "_scales")
+            nc.vector.quantize_mx(codes[:].bitcast(FP8X4), scales[:], values[:])
+            return codes, scales
 
-        quantise_w(0, (nc.scalar.copy, nc.scalar.copy))
+        w_bf0 = tile([P, PACK * H], BF16, "w_bf0")
+        for h in range(2):
+            round_w(nc.scalar.copy, w_bf0, w_raw0, h * HALF, (h + 1) * HALF)
 
         bias_col = tile([P, R // P], F32, "bias_col", tag="w_raw0")
         nc.scalar.copy(bias_col[:], bias_turned[:, P - 1 : BANK : P])
@@ -123,136 +127,152 @@ def tile_picked_yfism_lin_p_kernel(
                 bias_spread[:, c * P : (c + 1) * P], bias_col[:, c : c + 1].to_broadcast([P, P]), ident[:]
             )
         bias_all = tile([P, R], F32, "bias_all")
-
-        quantise_w(1, (nc.scalar.copy, nc.vector.tensor_copy))
         nc.scalar.copy(bias_all[:], bias_spread[:])
 
-        y = [[bank(CH_TILES * h + m, "y%d%d" % (h, m)) for m in range(CH_TILES)] for h in range(2)]
-        list_cols = HALF // 16
-        for o in range(2):
-            for h in range(2):
-                x_picked = tile([P, HALF], U32, "x_picked%d%d" % (o, h))
-                nc.vector.tensor_copy(x_picked[:], x_win[o][:].indirect(offs_sb[:, list_cols * h : list_cols * (h + 1)]))
-                for m in range(CH_TILES):
-                    nc.tensor.matmul_mx(
-                        out=y[h][m][:, 0:HALF],
-                        lhsT=w_codes[o][:, m * P : (m + 1) * P].bitcast(FP8X4),
-                        lhsT_scale=w_scales[o][:, m * P : (m + 1) * P],
-                        rhs=x_picked[:].bitcast(FP8X4),
-                        rhs_scale=x_plane[4 * o : P, h * HALF : (h + 1) * HALF],
-                        start=(o == 0),
-                        stop=(o == 1),
-                    )
+        x_picked = []
 
-        norm_col = tile([P, 2, 2], F32, "norm_col", tag="x_scale_win")
-        nc.scalar.dma_start(norm_col[:], norm[0, :].rearrange("(h c e) -> c h e", h=2, e=2))
-        out_tiles = out.rearrange("(h c e) g -> h e c g", h=2, e=2)
-        by_parity = {}
-        pair = {}
+        def gather_x(o):
+            x_picked.append(tile([P, S], U32, "x_picked%d" % o))
+            nc.vector.tensor_copy(by_item(x_picked[o]), x_win[o][:].indirect(offs_sb[:]))
 
-        def empty_y(h, m):
-            by_parity[h, m] = tile([P, 2, P], F32, "by_parity%d%d" % (h, m))
-            pair[h, m] = tile([P, P], F32, "pair%d%d" % (h, m))
-            src = y[h][m][:, 0:HALF]
-            pair_va = pair[h, m][:].rearrange("p (v a) -> p v a", a=2)
-            parity_va = by_parity[h, m][:].rearrange("p e (v a) -> p e v a", a=2)
-            if m == VECTOR_TILE:
-                nc.vector.tensor_reduce(pair[h, m][:], src.rearrange("p (c e) -> p c e", e=2), mybir.AxisListType.X, ADD)
-                nc.vector.tensor_tensor(
-                    parity_va,
-                    src.rearrange("p (v a e) -> p e v a", a=2, e=2),
-                    pair_va[:, :, ::-1].unsqueeze(1).to_broadcast([P, 2, P // 2, 2]),
-                    ADD,
+        alone = {d: bank(b, "y%d0" % d) for d, b in ((2, 4), (3, 5), (0, 0), (1, 1))}
+        paired = [bank(2 + e, "y%d1" % e) for e in range(2)]
+
+        def y(d, h):
+            if h == 0:
+                return alone[d][:, 0:HALF]
+            first = HALF if d < 2 else 0
+            return paired[d % 2][:, first : first + HALF]
+
+        def project(o, h, w_mx, first):
+            for d in ((2, 3, 0, 1), (2, 0, 3, 1))[h]:
+                nc.tensor.matmul_mx(
+                    out=y(d, h),
+                    lhsT=x_picked[o][:, d * P : (d + 1) * P].bitcast(FP8X4),
+                    lhsT_scale=x_plane[4 * o : P, d * P : (d + 1) * P],
+                    rhs=w_mx[0][:, first : first + HALF].bitcast(FP8X4),
+                    rhs_scale=w_mx[1][:, first : first + HALF],
+                    start=(o == 0 and (h == 0 or d >= 2)),
+                    stop=(o == 1 and (h == 0 or d < 2)),
                 )
-            else:
-                nc.scalar.copy(by_parity[h, m][:], src.rearrange("p (c e) -> p e c", e=2))
-                nc.vector.tensor_tensor(pair_va, parity_va[:, 0, :, ::-1], parity_va[:, 1, :, ::-1], ADD)
 
+        gather_x(0)
+        w_mx0 = quantise("w0", w_bf0, H)
+        for h in range(2):
+            project(0, h, w_mx0, h * HALF)
+        gather_x(1)
+        for h in range(2):
+            w_bf = tile([P, PACK * HALF], BF16, "w_bf1%d" % h, tag="w_raw0" if h == 0 else None)
+            round_w(nc.scalar.copy, w_bf, w_raw1[h], 0, SCALAR_COLS)
+            round_w(nc.vector.tensor_copy, w_bf, w_raw1[h], SCALAR_COLS, HALF)
+            project(1, h, quantise("w1%d" % h, w_bf, HALF), 0)
+
+        def dealt(bank_cols):
+            return bank_cols.rearrange("v (p u s) -> v u p s", u=2, s=2)
+
+        def shaped(t):
+            return t[:].rearrange("v (u p s) -> v u p s", u=2, s=2)
+
+        even = {}
+        pair = {}
         others = {}
-
-        def sum_others(h):
-            for e in range(2):
-                others[h, e] = bank(2 * h + e, "others%d%d" % (h, e))
-            early = [(m, e) for m in range(2) for e in range(2)]
-            late = [(m, e) for e in range(2) for m in range(2, CH_TILES)]
-            for m, e in early + late:
-                cols = others[h, e][:, m * P : (m + 1) * P]
-                opposite = by_parity[h, m][:, 1 - e, :]
-                if m == VECTOR_TILE:
-                    nc.tensor.transpose(cols, opposite, ident[:])
-                else:
-                    nc.tensor.matmul(cols, opposite, ident[:], is_transpose=True, start=True, stop=False)
-                    nc.tensor.matmul(cols, pair[h, m][:], ident[:], is_transpose=True, start=False, stop=True)
-
         z_rows = {}
-        z_cols = {}
-        scores = {}
 
-        def apply_norm(h, e):
-            z_rows[h, e] = tile([P, H], BF16, "z_rows%d%d" % (h, e))
-            dst = z_rows[h, e][:].rearrange("c (u p s) -> c u p s", u=2, s=2)
-            src = others[h, e][:].rearrange("c (p u s) -> c u p s", u=2, s=2)
-            if (h, e) == VECTOR_NORM:
-                nc.vector.tensor_scalar(dst, src, norm_col[:, h, e : e + 1], None, MULT)
+        def copy_even(d, h):
+            even[d, h] = tile([P, HALF], F32, "even%d%d" % (d, h))
+            nc.scalar.copy(shaped(even[d, h]), dealt(y(d, h)))
+
+        def sum_pair(d, h):
+            pair[d, h] = tile([P, HALF], F32, "pair%d%d" % (d, h))
+            nc.vector.tensor_tensor(shaped(pair[d, h]), dealt(y(d + 1, h)), shaped(even[d, h]), ADD)
+
+        def half_of(t, h):
+            return t[:].rearrange("v (u h q) -> v u h q", u=2, h=2)[:, :, h, :]
+
+        def by_u(t):
+            return t[:].rearrange("v (u q) -> v u q", u=2)
+
+        def sum_others(d, h):
+            far = pair[2 - d // 2 * 2, h]
+            others[d, h] = tile([P, HALF], F32, "others%d%d" % (d, h), tag="even21" if (d, h) == (1, 1) else None)
+            if d % 2 == 1:
+                nc.gpsimd.tensor_tensor(others[d, h][:], even[d - 1, h][:], far[:], ADD)
             else:
-                nc.scalar.activation(dst, src, COPY, scale=norm_col[:, h, e : e + 1])
+                nc.vector.tensor_tensor(shaped(others[d, h]), dealt(y(d + 1, h)), shaped(far), ADD)
 
-        def turn(h, e):
-            turned = bank(CH_TILES + 2 * h + e, "turned%d%d" % (h, e))
-            pairs = z_rows[h, e][:].bitcast(F32)
+        def apply_norm(d, h=None):
+            factor = norm_col[:, d : d + 1]
+            if h == 0:
+                z_rows[d] = tile([P, H], BF16, "z_rows%d" % d)
+            if (d, h) == (1, 1):
+                nc.gpsimd.tensor_scalar(half_of(z_rows[d], h), by_u(others[d, h]), factor, 0.0, MULT, ADD)
+            else:
+                nc.scalar.activation(half_of(z_rows[d], h), by_u(others[d, h]), COPY, scale=factor)
+
+        z_cols = {}
+        turned = {}
+
+        def turn(d):
+            turned[d] = bank((6, 6, 7, 4)[d], "turned%d" % d)
+            pairs = z_rows[d][:].bitcast(F32)
             for u in range(2):
-                nc.tensor.transpose(turned[:, u * P : (u + 1) * P], pairs[:, u * P : (u + 1) * P], ident[:])
-            z_cols[h, e] = tile([P, P * PACK], BF16, "z_cols%d%d" % (h, e))
+                nc.tensor.transpose(turned[d][:, u * P : (u + 1) * P], pairs[:, u * P : (u + 1) * P], ident[:])
+
+        def copy_turned(d):
+            z_cols[d] = tile([P, P * PACK], BF16, "z_cols%d" % d)
             nc.scalar.copy(
-                z_cols[h, e][:].bitcast(F32).rearrange("p (c u) -> p c u", u=2),
-                turned[:, 0 : 2 * P].rearrange("p (u c) -> p c u", u=2),
+                z_cols[d][:].bitcast(F32).rearrange("p (c u) -> p c u", u=2),
+                turned[d][:, 0 : 2 * P].rearrange("p (u c) -> p c u", u=2),
             )
 
-        codes = {}
+        out_tiles = out.rearrange("(v d) g -> d v g", d=D)
+        z_mx = {}
 
-        def quantise_z(h, e):
-            z_codes = tile([P, P], U32, "z_codes%d%d" % (h, e))
-            z_scales = tile([P, P], U8, "z_scales%d%d" % (h, e))
-            nc.vector.quantize_mx(z_codes[:].bitcast(FP8X4), z_scales[:], z_cols[h, e][:])
-            codes[h, e] = (z_codes, z_scales)
+        def quantise_z(d):
+            z_mx[d] = quantise("z%d" % d, z_cols[d], P)
 
-        def score(h, e, a, b, on_bank):
-            scores[h, e, a] = bank(on_bank, "scores%d%d%d" % (h, e, a))
+        def score(d, a, b, on_bank):
+            scores = bank(on_bank, "scores%d%d" % (d, a))
             nc.tensor.matmul_mx(
-                out=scores[h, e, a][:, 0 : b - a],
-                lhsT=codes[h, e][0][:].bitcast(FP8X4),
-                lhsT_scale=codes[h, e][1][:],
+                out=scores[:, 0 : b - a],
+                lhsT=z_mx[d][0][:].bitcast(FP8X4),
+                lhsT_scale=z_mx[d][1][:],
                 rhs=v_picked[:, a:b].bitcast(FP8X4),
                 rhs_scale=v_plane[:, a:b],
                 start=True,
                 stop=True,
             )
+            return scores[:, 0 : b - a]
 
-        def store(h, e, a, b, first):
-            result = tile([P, b - a], F32, "result%d%d%d" % (h, e, a))
-            nc.vector.tensor_tensor(result[:], scores[h, e, first][:, a - first : b - first], bias_all[:, a:b], ADD)
-            nc.sync.dma_start(out_tiles[h, e, :, a:b], result[:])
+        def store(d, a, scores):
+            b = a + scores.shape[1]
+            result = tile([P, b - a], F32, "result%d%d" % (d, a))
+            nc.vector.tensor_tensor(result[:], scores, bias_all[:, a:b], ADD)
+            nc.sync.dma_start(out_tiles[d, :, a:b], result[:])
 
         for h in range(2):
-            for m in range(CH_TILES):
-                empty_y(h, m)
-        v_picked = tile([P, R], U32, "v_picked")
+            for d in (2, 0):
+                copy_even(d, h)
+            sum_pair(2, h)
+            sum_pair(0, h)
+            for d in (0, 3, 1):
+                sum_others(d, h)
+        for h in range(2):
+            sum_others(2, h)
+        for d, h in ((0, 0), (2, 0), (1, 0), (3, 0), (0, 1), (2, 1), (3, 1), (1, 1)):
+            apply_norm(d, h)
+        v_picked = tile([P, R], U32, "v_picked", tag="pair01")
         nc.vector.tensor_copy(v_picked[:], v_win[:].indirect(items_sb[:]))
-        for h in range(2):
-            sum_others(h)
-        tiles = [(h, e) for h in range(2) for e in range(2)]
-        for stage in (apply_norm, turn):
-            for h, e in tiles:
-                stage(h, e)
-        quantise_z(0, 0)
-        score(0, 0, 0, R // 2, 0)
-        score(0, 0, R // 2, R, CH_TILES)
-        for h, e in tiles[1:3]:
-            quantise_z(h, e)
-            score(h, e, 0, R, 2 * h + e)
-        store(0, 0, 0, R // 2, 0)
-        quantise_z(1, 1)
-        score(1, 1, 0, R, 3)
-        store(0, 0, R // 2, R, R // 2)
-        for h, e in tiles[1:]:
-            store(h, e, 0, R, 0)
+        ORDER = (0, 2, 3, 1)
+        for d in ORDER:
+            turn(d)
+            copy_turned(d)
+        for d in ORDER[0:3]:
+            quantise_z(d)
+        store(0, 0, score(0, 0, R, 0))
+        quantise_z(1)
+        for d, on_bank in ((2, 1), (3, 2)):
+            store(d, 0, score(d, 0, R, on_bank))
+        last = score(1, 0, R, 5)
+        for a in (0, R // 2):
+            store(1, a, last[:, a : a + R // 2])

@@ -16,6 +16,7 @@ FP8X4 = mybir.dt.float8_e4m3fn_x4
 COPY = mybir.ActivationFunctionType.Copy
 MULT = mybir.AluOpType.mult
 ADD = mybir.AluOpType.add
+SUB = mybir.AluOpType.subtract
 
 P = 128
 PACK = 4
@@ -115,9 +116,9 @@ def tile_picked_yfism_lin_p_kernel(
             nc.vector.quantize_mx(codes[:].bitcast(FP8X4), scales[:], values[:])
             return codes, scales
 
-        w_bf0 = tile([P, PACK * H], BF16, "w_bf0")
+        w_bf0 = [tile([P, PACK * HALF], BF16, "w_bf0%d" % h) for h in range(2)]
         for h in range(2):
-            round_w(nc.scalar.copy, w_bf0, w_raw0, h * HALF, (h + 1) * HALF)
+            round_w(nc.scalar.copy, w_bf0[h], w_raw0[:, :, h * HALF : (h + 1) * HALF], 0, HALF)
 
         bias_col = tile([P, R // P], F32, "bias_col", tag="w_raw0")
         nc.scalar.copy(bias_col[:], bias_turned[:, P - 1 : BANK : P])
@@ -136,36 +137,49 @@ def tile_picked_yfism_lin_p_kernel(
             nc.vector.tensor_copy(by_item(x_picked[o]), x_win[o][:].indirect(offs_sb[:]))
 
         alone = {d: bank(b, "y%d0" % d) for d, b in ((2, 4), (3, 5), (0, 0), (1, 1))}
-        paired = [bank(2 + e, "y%d1" % e) for e in range(2)]
+        paired = [bank(2 + e, "pair_bank%d" % e) for e in range(2)]
+        direct = bank(6, "direct")
+        PLACE = {0: (0, 0), 1: (0, HALF), 2: (1, 0), 3: (1, HALF)}
 
         def y(d, h):
             if h == 0:
                 return alone[d][:, 0:HALF]
-            first = HALF if d < 2 else 0
-            return paired[d % 2][:, first : first + HALF]
+            e, first = PLACE[d]
+            return paired[e][:, first : first + HALF]
 
-        def project(o, h, w_mx, first):
-            for d in ((2, 3, 0, 1), (2, 0, 3, 1))[h]:
-                nc.tensor.matmul_mx(
-                    out=y(d, h),
-                    lhsT=x_picked[o][:, d * P : (d + 1) * P].bitcast(FP8X4),
-                    lhsT_scale=x_plane[4 * o : P, d * P : (d + 1) * P],
-                    rhs=w_mx[0][:, first : first + HALF].bitcast(FP8X4),
-                    rhs_scale=w_mx[1][:, first : first + HALF],
-                    start=(o == 0 and (h == 0 or d >= 2)),
-                    stop=(o == 1 and (h == 0 or d < 2)),
-                )
+        def project(o, d, w_mx, first, cols, opens, closes):
+            nc.tensor.matmul_mx(
+                out=cols,
+                lhsT=x_picked[o][:, d * P : (d + 1) * P].bitcast(FP8X4),
+                lhsT_scale=x_plane[4 * o : P, d * P : (d + 1) * P],
+                rhs=w_mx[0][:, first : first + HALF].bitcast(FP8X4),
+                rhs_scale=w_mx[1][:, first : first + HALF],
+                start=(o == 0 and opens),
+                stop=(o == 1 and closes),
+            )
 
+        def project_half(o, h, w_mx, first):
+            if h == 0:
+                for d in (2, 3, 0, 1):
+                    project(o, d, w_mx, first, y(d, 0), True, True)
+                return
+            for d in (0, 1):
+                project(o, d, w_mx, first, y(d, 1), d == 0, d == 1)
+            for d in (1, 2, 3):
+                project(o, d, w_mx, first, direct[:, 0:HALF], d == 1, d == 3)
+            for d in (2, 3):
+                project(o, d, w_mx, first, y(d, 1), d == 2, d == 3)
+
+        w_mx00 = quantise("w00", w_bf0[0], HALF)
         gather_x(0)
-        w_mx0 = quantise("w0", w_bf0, H)
-        for h in range(2):
-            project(0, h, w_mx0, h * HALF)
+        project_half(0, 0, w_mx00, 0)
+        project_half(0, 1, quantise("w01", w_bf0[1], HALF), 0)
         gather_x(1)
         for h in range(2):
             w_bf = tile([P, PACK * HALF], BF16, "w_bf1%d" % h, tag="w_raw0" if h == 0 else None)
             round_w(nc.scalar.copy, w_bf, w_raw1[h], 0, SCALAR_COLS)
             round_w(nc.vector.tensor_copy, w_bf, w_raw1[h], SCALAR_COLS, HALF)
-            project(1, h, quantise("w1%d" % h, w_bf, HALF), 0)
+            project_half(1, h, quantise("w1%d" % h, w_bf, HALF), 0)
 
         def dealt(bank_cols):
             return bank_cols.rearrange("v (p u s) -> v u p s", u=2, s=2)
@@ -173,47 +187,46 @@ def tile_picked_yfism_lin_p_kernel(
         def shaped(t):
             return t[:].rearrange("v (u p s) -> v u p s", u=2, s=2)
 
-        even = {}
-        pair = {}
+        def half_tile(name, tag=None):
+            return tile([P, HALF], F32, name, tag=tag)
+
+        def copy_y(d, h):
+            copy = half_tile("copy%d%d" % (d, h))
+            nc.scalar.copy(shaped(copy), dealt(y(d, h)))
+            return copy
+
+        def combine(name, sbuf, psum, op):
+            made = half_tile(name)
+            nc.vector.tensor_tensor(shaped(made), shaped(sbuf), dealt(psum), op)
+            return made
+
+        def combine_copies(name, left, right, op):
+            made = half_tile(name)
+            nc.gpsimd.tensor_tensor(made[:], left[:], right[:], op)
+            return made
+
         others = {}
         z_rows = {}
 
-        def copy_even(d, h):
-            even[d, h] = tile([P, HALF], F32, "even%d%d" % (d, h))
-            nc.scalar.copy(shaped(even[d, h]), dealt(y(d, h)))
-
-        def sum_pair(d, h):
-            pair[d, h] = tile([P, HALF], F32, "pair%d%d" % (d, h))
-            nc.vector.tensor_tensor(shaped(pair[d, h]), dealt(y(d + 1, h)), shaped(even[d, h]), ADD)
-
-        def half_of(t, h):
-            return t[:].rearrange("v (u h q) -> v u h q", u=2, h=2)[:, :, h, :]
-
-        def by_u(t):
-            return t[:].rearrange("v (u q) -> v u q", u=2)
-
-        def sum_others(d, h):
-            far = pair[2 - d // 2 * 2, h]
-            others[d, h] = tile([P, HALF], F32, "others%d%d" % (d, h), tag="even21" if (d, h) == (1, 1) else None)
-            if d % 2 == 1:
-                nc.gpsimd.tensor_tensor(others[d, h][:], even[d - 1, h][:], far[:], ADD)
-            else:
-                nc.vector.tensor_tensor(shaped(others[d, h]), dealt(y(d + 1, h)), shaped(far), ADD)
-
-        def apply_norm(d, h=None):
+        def apply_norm(d, h):
             factor = norm_col[:, d : d + 1]
             if h == 0:
                 z_rows[d] = tile([P, H], BF16, "z_rows%d" % d)
-            if (d, h) == (1, 1):
-                nc.gpsimd.tensor_scalar(half_of(z_rows[d], h), by_u(others[d, h]), factor, 0.0, MULT, ADD)
+            dst = z_rows[d][:].rearrange("v (u h q) -> v u h q", u=2, h=2)[:, :, h, :]
+            if (d, h) == (0, 1):
+                nc.scalar.activation(dst.rearrange("v u (p s) -> v u p s", s=2), dealt(direct[:, 0:HALF]), COPY, scale=factor)
+                return
+            src = others[d, h][:].rearrange("v (u q) -> v u q", u=2)
+            if h == 0 and d % 2 == 1:
+                nc.gpsimd.tensor_scalar(dst, src, factor, 0.0, MULT, ADD)
             else:
-                nc.scalar.activation(half_of(z_rows[d], h), by_u(others[d, h]), COPY, scale=factor)
+                nc.scalar.activation(dst, src, COPY, scale=factor)
 
         z_cols = {}
         turned = {}
 
         def turn(d):
-            turned[d] = bank((6, 6, 7, 4)[d], "turned%d" % d)
+            turned[d] = bank((7, 7, 4, 0)[d], "turned%d" % d)
             pairs = z_rows[d][:].bitcast(F32)
             for u in range(2):
                 nc.tensor.transpose(turned[d][:, u * P : (u + 1) * P], pairs[:, u * P : (u + 1) * P], ident[:])
@@ -231,18 +244,26 @@ def tile_picked_yfism_lin_p_kernel(
         def quantise_z(d):
             z_mx[d] = quantise("z%d" % d, z_cols[d], P)
 
-        def score(d, a, b, on_bank):
-            scores = bank(on_bank, "scores%d%d" % (d, a))
-            nc.tensor.matmul_mx(
-                out=scores[:, 0 : b - a],
-                lhsT=z_mx[d][0][:].bitcast(FP8X4),
-                lhsT_scale=z_mx[d][1][:],
-                rhs=v_picked[:, a:b].bitcast(FP8X4),
-                rhs_scale=v_plane[:, a:b],
-                start=True,
-                stop=True,
-            )
-            return scores[:, 0 : b - a]
+        COLS = R // 2
+        v_picked = []
+
+        def gather_v(n, tag):
+            v_picked.append(tile([P, COLS], U32, "v_picked%d" % n, tag=tag))
+            nc.vector.tensor_copy(v_picked[n][:], v_win[:].indirect(items_sb[:, 16 * n : 16 * (n + 1)]))
+
+        def score(d, halves, on_bank):
+            scores = bank(on_bank, "scores%d%d" % (d, halves[0]))
+            for i, n in enumerate(halves):
+                nc.tensor.matmul_mx(
+                    out=scores[:, i * COLS : (i + 1) * COLS],
+                    lhsT=z_mx[d][0][:].bitcast(FP8X4),
+                    lhsT_scale=z_mx[d][1][:],
+                    rhs=v_picked[n][:].bitcast(FP8X4),
+                    rhs_scale=v_plane[:, n * COLS : (n + 1) * COLS],
+                    start=True,
+                    stop=True,
+                )
+            return scores[:, 0 : len(halves) * COLS]
 
         def store(d, a, scores):
             b = a + scores.shape[1]
@@ -250,29 +271,39 @@ def tile_picked_yfism_lin_p_kernel(
             nc.vector.tensor_tensor(result[:], scores, bias_all[:, a:b], ADD)
             nc.sync.dma_start(out_tiles[d, :, a:b], result[:])
 
-        for h in range(2):
-            for d in (2, 0):
-                copy_even(d, h)
-            sum_pair(2, h)
-            sum_pair(0, h)
-            for d in (0, 3, 1):
-                sum_others(d, h)
-        for h in range(2):
-            sum_others(2, h)
-        for d, h in ((0, 0), (2, 0), (1, 0), (3, 0), (0, 1), (2, 1), (3, 1), (1, 1)):
+        y2 = copy_y(2, 0)
+        y0 = copy_y(0, 0)
+        far = combine("pair23", y2, y(3, 0), ADD)
+        near = combine("pair01", y0, y(1, 0), ADD)
+        others[0, 0] = combine("others00", far, y(1, 0), ADD)
+        others[2, 0] = combine("others20", near, y(3, 0), ADD)
+        others[1, 0] = combine_copies("others10", y0, far, ADD)
+        others[3, 0] = combine_copies("others30", y2, near, ADD)
+
+        whole = combine("whole", copy_y(0, 1), direct[:, 0:HALF], ADD)
+        for d in (2, 3, 1):
+            others[d, 1] = combine("others%d1" % d, whole, y(d, 1), SUB)
+        gather_v(0, "copy01")
+        for d, h in ((3, 0), (1, 0), (0, 0), (0, 1), (2, 0), (2, 1), (3, 1)):
             apply_norm(d, h)
-        v_picked = tile([P, R], U32, "v_picked", tag="pair01")
-        nc.vector.tensor_copy(v_picked[:], v_win[:].indirect(items_sb[:]))
-        ORDER = (0, 2, 3, 1)
-        for d in ORDER:
+        turn(0)
+        copy_turned(0)
+        apply_norm(1, 1)
+        quantise_z(0)
+        gather_v(1, "z_cols0")
+        for d in (2, 3):
             turn(d)
             copy_turned(d)
-        for d in ORDER[0:3]:
-            quantise_z(d)
-        store(0, 0, score(0, 0, R, 0))
+        first = score(0, (0,), 1)
+        turn(1)
+        copy_turned(1)
+        second = score(0, (1,), 5)
+        quantise_z(2)
+        quantise_z(3)
+        store(0, 0, first)
         quantise_z(1)
-        for d, on_bank in ((2, 1), (3, 2)):
-            store(d, 0, score(d, 0, R, on_bank))
-        last = score(1, 0, R, 5)
-        for a in (0, R // 2):
-            store(1, a, last[:, a : a + R // 2])
+        store(0, COLS, second)
+        for d, on_bank in ((2, 2), (3, 3)):
+            store(d, 0, score(d, (0, 1), on_bank))
+        for n, on_bank in enumerate((6, 4)):
+            store(1, n * COLS, score(1, (n,), on_bank))

@@ -36,6 +36,7 @@ def tile_picked_yfism_lin_p_kernel(
     nc = tc.nc
     with ExitStack() as ctx:
         sb = ctx.enter_context(tc.tile_pool(name="sb", bufs=1))
+        shared = ctx.enter_context(tc.tile_pool(name="shared", bufs=1))
         ps = ctx.enter_context(tc.psum_pool(name="ps", bufs=1))
 
         def bank(b, name):
@@ -48,7 +49,7 @@ def tile_picked_yfism_lin_p_kernel(
         items_sb = tile([P, R // 16], U16, "items_sb")
         x_scale_win = tile([P, T], U8, "x_scale_win")
         v_scale_win = tile([P, G], U8, "v_scale_win")
-        bias_win = tile([P, G], F32, "bias_win")
+        bias_win = shared.tile([P, G], F32, name="bias_win", align_bytes=64, offset=0)
         nc.gpsimd.memset(x_scale_win[0:X_ROWS, :].bitcast(I32), 0)
         nc.vector.memset(bias_win[0 : P - 1, :], 0.0)
         x_plane = tile([P, S], U8, "x_plane")
@@ -94,17 +95,17 @@ def tile_picked_yfism_lin_p_kernel(
         place_scales(x_plane, 4, x_scale_picked, X_ROWS + BLOCKS)
         w_raw1 = []
         w_raw1.append(tile([P, PACK, HALF], F32, "w_raw10", tag="v_scale_win"))
-        w_raw1.append(tile([P, PACK, HALF], F32, "w_raw11", tag="bias_win"))
+        w_raw1.append(shared.tile([P, PACK, HALF], F32, name="w_raw11", align_bytes=64, offset=0))
         for h in range(2):
             nc.sync.dma_start(w_raw1[h][:], w1[PASS:K, h * HALF : (h + 1) * HALF].rearrange("(p j) c -> p j c", j=PACK))
+        norm_col = shared.tile([P, D], F32, name="norm_col", align_bytes=64, offset=4 * PACK * HALF)
+        nc.sync.dma_start(norm_col[:], norm[0, :].rearrange("(v d) -> v d", d=D))
 
         bias_turned = bank(7, "bias_turned")
         for c in range(R // P):
             nc.tensor.transpose(bias_turned[:, c * P : (c + 1) * P], bias_picked[:, c * P : (c + 1) * P], ident[:])
         v_win = load_words("v_win", "bias_picked", v_words[0])
         place_scales(v_plane, 0, v_scale_picked, V_ROWS)
-        norm_col = tile([P, D], F32, "norm_col", tag="x_scale_picked")
-        nc.sync.dma_start(norm_col[:], norm[0, :].rearrange("(v d) -> v d", d=D))
 
         def round_w(copy, w_bf, raw, a, b):
             dst = w_bf[:, PACK * a : PACK * b]
@@ -187,6 +188,9 @@ def tile_picked_yfism_lin_p_kernel(
         def shaped(t):
             return t[:].rearrange("v (u p s) -> v u p s", u=2, s=2)
 
+        def by_u(t):
+            return t[:].rearrange("v (u q) -> v u q", u=2)
+
         def half_tile(name, tag=None):
             return tile([P, HALF], F32, name, tag=tag)
 
@@ -210,6 +214,10 @@ def tile_picked_yfism_lin_p_kernel(
 
         def apply_norm(d, h):
             factor = norm_col[:, d : d + 1]
+            if d == 1:
+                z_rows[1] = tile([P, H], BF16, "z_rows1", tag="z_rows0")
+                nc.scalar.activation(z_rows[1][:], last_others[:], COPY, scale=factor)
+                return
             if h == 0:
                 z_rows[d] = tile([P, H], BF16, "z_rows%d" % d)
             dst = z_rows[d][:].rearrange("v (u h q) -> v u h q", u=2, h=2)[:, :, h, :]
@@ -217,7 +225,7 @@ def tile_picked_yfism_lin_p_kernel(
                 nc.scalar.activation(dst.rearrange("v u (p s) -> v u p s", s=2), dealt(direct[:, 0:HALF]), COPY, scale=factor)
                 return
             src = others[d, h][:].rearrange("v (u q) -> v u q", u=2)
-            if h == 0 and d % 2 == 1:
+            if (d, h) == (3, 0):
                 nc.gpsimd.tensor_scalar(dst, src, factor, 0.0, MULT, ADD)
             else:
                 nc.scalar.activation(dst, src, COPY, scale=factor)
@@ -277,18 +285,23 @@ def tile_picked_yfism_lin_p_kernel(
         near = combine("pair01", y0, y(1, 0), ADD)
         others[0, 0] = combine("others00", far, y(1, 0), ADD)
         others[2, 0] = combine("others20", near, y(3, 0), ADD)
-        others[1, 0] = combine_copies("others10", y0, far, ADD)
+        last_others = tile([P, H], F32, "others1")
+        last_halves = last_others[:].rearrange("v (u h q) -> v h u q", u=2, h=2)
+        nc.gpsimd.tensor_tensor(last_halves[:, 0], by_u(y0), by_u(far), ADD)
         others[3, 0] = combine_copies("others30", y2, near, ADD)
 
         whole = combine("whole", copy_y(0, 1), direct[:, 0:HALF], ADD)
-        for d in (2, 3, 1):
+        for d in (2, 3):
             others[d, 1] = combine("others%d1" % d, whole, y(d, 1), SUB)
+        nc.vector.tensor_tensor(
+            last_halves[:, 1].rearrange("v u (p s) -> v u p s", s=2), shaped(whole), dealt(y(1, 1)), SUB
+        )
         gather_v(0, "copy01")
-        for d, h in ((3, 0), (1, 0), (0, 0), (0, 1), (2, 0), (2, 1), (3, 1)):
+        for d, h in ((3, 0), (0, 0), (2, 0), (0, 1), (2, 1), (3, 1)):
             apply_norm(d, h)
         turn(0)
         copy_turned(0)
-        apply_norm(1, 1)
+        apply_norm(1, None)
         quantise_z(0)
         gather_v(1, "z_cols0")
         for d in (2, 3):

@@ -215,7 +215,7 @@ def tile_picked_yfism_lin_p_kernel(
         def apply_norm(d, h):
             factor = norm_col[:, d : d + 1]
             if d == 1:
-                z_rows[1] = tile([P, H], BF16, "z_rows1", tag="z_rows0")
+                z_rows[1] = tile([P, H], BF16, "z_rows1", tag="others21")
                 nc.scalar.activation(z_rows[1][:], last_others[:], COPY, scale=factor)
                 return
             if h == 0:
@@ -234,7 +234,7 @@ def tile_picked_yfism_lin_p_kernel(
         turned = {}
 
         def turn(d):
-            turned[d] = bank((7, 7, 4, 0)[d], "turned%d" % d)
+            turned[d] = bank((7, 5, 4, 0)[d], "turned%d" % d)
             pairs = z_rows[d][:].bitcast(F32)
             for u in range(2):
                 nc.tensor.transpose(turned[d][:, u * P : (u + 1) * P], pairs[:, u * P : (u + 1) * P], ident[:])
@@ -253,25 +253,19 @@ def tile_picked_yfism_lin_p_kernel(
             z_mx[d] = quantise("z%d" % d, z_cols[d], P)
 
         COLS = R // 2
-        v_picked = []
 
-        def gather_v(n, tag):
-            v_picked.append(tile([P, COLS], U32, "v_picked%d" % n, tag=tag))
-            nc.vector.tensor_copy(v_picked[n][:], v_win[:].indirect(items_sb[:, 16 * n : 16 * (n + 1)]))
-
-        def score(d, halves, on_bank):
-            scores = bank(on_bank, "scores%d%d" % (d, halves[0]))
-            for i, n in enumerate(halves):
-                nc.tensor.matmul_mx(
-                    out=scores[:, i * COLS : (i + 1) * COLS],
-                    lhsT=z_mx[d][0][:].bitcast(FP8X4),
-                    lhsT_scale=z_mx[d][1][:],
-                    rhs=v_picked[n][:].bitcast(FP8X4),
-                    rhs_scale=v_plane[:, n * COLS : (n + 1) * COLS],
-                    start=True,
-                    stop=True,
-                )
-            return scores[:, 0 : len(halves) * COLS]
+        def score(d, a, b, on_bank):
+            scores = bank(on_bank, "scores%d%d" % (d, a))
+            nc.tensor.matmul_mx(
+                out=scores[:, 0 : b - a],
+                lhsT=z_mx[d][0][:].bitcast(FP8X4),
+                lhsT_scale=z_mx[d][1][:],
+                rhs=v_picked[:, a:b].bitcast(FP8X4),
+                rhs_scale=v_plane[:, a:b],
+                start=True,
+                stop=True,
+            )
+            return scores[:, 0 : b - a]
 
         def store(d, a, scores):
             b = a + scores.shape[1]
@@ -296,27 +290,15 @@ def tile_picked_yfism_lin_p_kernel(
         nc.vector.tensor_tensor(
             last_halves[:, 1].rearrange("v u (p s) -> v u p s", s=2), shaped(whole), dealt(y(1, 1)), SUB
         )
-        gather_v(0, "copy01")
-        for d, h in ((3, 0), (0, 0), (2, 0), (0, 1), (2, 1), (3, 1)):
+        v_picked = tile([P, R], U32, "v_picked", tag="copy01")
+        nc.vector.tensor_copy(v_picked[:], v_win[:].indirect(items_sb[:]))
+        for d, h in ((3, 0), (0, 0), (2, 0), (0, 1), (2, 1), (3, 1), (1, None)):
             apply_norm(d, h)
-        turn(0)
-        copy_turned(0)
-        apply_norm(1, None)
-        quantise_z(0)
-        gather_v(1, "z_cols0")
-        for d in (2, 3):
+        for d in (0, 2, 3, 1):
             turn(d)
             copy_turned(d)
-        first = score(0, (0,), 1)
-        turn(1)
-        copy_turned(1)
-        second = score(0, (1,), 5)
-        quantise_z(2)
-        quantise_z(3)
-        store(0, 0, first)
-        quantise_z(1)
-        store(0, COLS, second)
-        for d, on_bank in ((2, 2), (3, 3)):
-            store(d, 0, score(d, (0, 1), on_bank))
-        for n, on_bank in enumerate((6, 4)):
-            store(1, n * COLS, score(1, (n,), on_bank))
+            quantise_z(d)
+        for d, on_bank in ((0, 1), (2, 2), (3, 3)):
+            store(d, 0, score(d, 0, R, on_bank))
+        for a, on_bank in ((0, 7), (COLS, 4)):
+            store(1, a, score(1, a, a + COLS, on_bank))

@@ -137,16 +137,15 @@ def tile_picked_yfism_lin_p_kernel(
             x_picked.append(tile([P, S], U32, "x_picked%d" % o))
             nc.vector.tensor_copy(by_item(x_picked[o]), x_win[o][:].indirect(offs_sb[:]))
 
-        alone = {d: bank(b, "y%d0" % d) for d, b in ((2, 4), (3, 5), (0, 0), (1, 1))}
-        paired = [bank(2 + e, "pair_bank%d" % e) for e in range(2)]
+        alone = {(d, 0): bank(b, "y%d0" % d) for d, b in ((2, 4), (3, 5), (0, 0), (1, 1))}
+        alone.update({(d, 1): bank(b, "y%d1" % d) for d, b in ((0, 2), (1, 7))})
+        paired = bank(3, "y231")
         direct = bank(6, "direct")
-        PLACE = {0: (0, 0), 1: (0, HALF), 2: (1, 0), 3: (1, HALF)}
 
         def y(d, h):
-            if h == 0:
-                return alone[d][:, 0:HALF]
-            e, first = PLACE[d]
-            return paired[e][:, first : first + HALF]
+            if (d, h) in alone:
+                return alone[d, h][:, 0:HALF]
+            return paired[:, (d - 2) * HALF : (d - 1) * HALF]
 
         def project(o, d, w_mx, first, cols, opens, closes):
             nc.tensor.matmul_mx(
@@ -164,12 +163,12 @@ def tile_picked_yfism_lin_p_kernel(
                 for d in (2, 3, 0, 1):
                     project(o, d, w_mx, first, y(d, 0), True, True)
                 return
-            for d in (0, 1):
-                project(o, d, w_mx, first, y(d, 1), d == 0, d == 1)
+            project(o, 0, w_mx, first, y(0, 1), True, True)
             for d in (1, 2, 3):
                 project(o, d, w_mx, first, direct[:, 0:HALF], d == 1, d == 3)
             for d in (2, 3):
                 project(o, d, w_mx, first, y(d, 1), d == 2, d == 3)
+            project(o, 1, w_mx, first, y(1, 1), True, True)
 
         w_mx00 = quantise("w00", w_bf0[0], HALF)
         gather_x(0)
@@ -199,8 +198,8 @@ def tile_picked_yfism_lin_p_kernel(
             nc.scalar.copy(shaped(copy), dealt(y(d, h)))
             return copy
 
-        def combine(name, sbuf, psum, op):
-            made = half_tile(name)
+        def combine(name, sbuf, psum, op, tag=None):
+            made = half_tile(name, tag)
             nc.vector.tensor_tensor(shaped(made), shaped(sbuf), dealt(psum), op)
             return made
 
@@ -234,7 +233,7 @@ def tile_picked_yfism_lin_p_kernel(
         turned = {}
 
         def turn(d):
-            turned[d] = bank((7, 5, 4, 0)[d], "turned%d" % d)
+            turned[d] = bank((4, 5, 1, 0)[d], "turned%d" % d)
             pairs = z_rows[d][:].bitcast(F32)
             for u in range(2):
                 nc.tensor.transpose(turned[d][:, u * P : (u + 1) * P], pairs[:, u * P : (u + 1) * P], ident[:])
@@ -298,7 +297,7 @@ def tile_picked_yfism_lin_p_kernel(
             turn(d)
             copy_turned(d)
             quantise_z(d)
-        for d, on_bank in ((0, 1), (2, 2), (3, 3)):
+        for d, on_bank in ((0, 2), (2, 6), (3, 3)):
             store(d, 0, score(d, 0, R, on_bank))
         for a, on_bank in ((0, 7), (COLS, 4)):
             store(1, a, score(1, a, a + COLS, on_bank))

@@ -138,14 +138,14 @@ def tile_picked_yfism_lin_p_kernel(
             nc.vector.tensor_copy(by_item(x_picked[o]), x_win[o][:].indirect(offs_sb[:]))
 
         alone = {(d, 0): bank(b, "y%d0" % d) for d, b in ((2, 4), (3, 5), (0, 0), (1, 1))}
-        alone.update({(d, 1): bank(b, "y%d1" % d) for d, b in ((0, 2), (1, 7))})
-        paired = bank(3, "y231")
+        alone.update({(d, 1): bank(b, "y%d1" % d) for d, b in ((0, 2), (2, 3))})
+        paired = []
         direct = bank(6, "direct")
 
         def y(d, h):
             if (d, h) in alone:
                 return alone[d, h][:, 0:HALF]
-            return paired[:, (d - 2) * HALF : (d - 1) * HALF]
+            return paired[0][:, d // 2 * HALF : (d // 2 + 1) * HALF]
 
         def project(o, d, w_mx, first, cols, opens, closes):
             nc.tensor.matmul_mx(
@@ -166,20 +166,21 @@ def tile_picked_yfism_lin_p_kernel(
             project(o, 0, w_mx, first, y(0, 1), True, True)
             for d in (1, 2, 3):
                 project(o, d, w_mx, first, direct[:, 0:HALF], d == 1, d == 3)
-            for d in (2, 3):
-                project(o, d, w_mx, first, y(d, 1), d == 2, d == 3)
-            project(o, 1, w_mx, first, y(1, 1), True, True)
+            project(o, 2, w_mx, first, y(2, 1), True, True)
 
         w_mx00 = quantise("w00", w_bf0[0], HALF)
         gather_x(0)
         project_half(0, 0, w_mx00, 0)
-        project_half(0, 1, quantise("w01", w_bf0[1], HALF), 0)
+        second = [quantise("w01", w_bf0[1], HALF)]
+        project_half(0, 1, second[0], 0)
         gather_x(1)
         for h in range(2):
             w_bf = tile([P, PACK * HALF], BF16, "w_bf1%d" % h, tag="w_raw0" if h == 0 else None)
             round_w(nc.scalar.copy, w_bf, w_raw1[h], 0, SCALAR_COLS)
             round_w(nc.vector.tensor_copy, w_bf, w_raw1[h], SCALAR_COLS, HALF)
-            project_half(1, h, quantise("w1%d" % h, w_bf, HALF), 0)
+            w_mx = quantise("w1%d" % h, w_bf, HALF)
+            project_half(1, h, w_mx, 0)
+        second.append(w_mx)
 
         def dealt(bank_cols):
             return bank_cols.rearrange("v (p u s) -> v u p s", u=2, s=2)
@@ -284,6 +285,10 @@ def tile_picked_yfism_lin_p_kernel(
         others[3, 0] = combine_copies("others30", y2, near, ADD)
 
         whole = combine("whole", copy_y(0, 1), direct[:, 0:HALF], ADD)
+        paired.append(bank(2, "y_odd"))
+        for d in (3, 1):
+            for o in range(2):
+                project(o, d, second[o], 0, y(d, 1), d == 3, d == 1)
         for d in (2, 3):
             others[d, 1] = combine("others%d1" % d, whole, y(d, 1), SUB)
         nc.vector.tensor_tensor(
@@ -297,7 +302,7 @@ def tile_picked_yfism_lin_p_kernel(
             turn(d)
             copy_turned(d)
             quantise_z(d)
-        for d, on_bank in ((0, 2), (2, 6), (3, 3)):
+        for d, on_bank in ((0, 7), (2, 6), (3, 3)):
             store(d, 0, score(d, 0, R, on_bank))
-        for a, on_bank in ((0, 7), (COLS, 4)):
+        for a, on_bank in ((0, 2), (COLS, 4)):
             store(1, a, score(1, a, a + COLS, on_bank))

@@ -214,10 +214,6 @@ def tile_picked_yfism_lin_p_kernel(
 
         def apply_norm(d, h):
             factor = norm_col[:, d : d + 1]
-            if d == 1:
-                z_rows[1] = tile([P, H], BF16, "z_rows1", tag="others21")
-                nc.scalar.activation(z_rows[1][:], last_others[:], COPY, scale=factor)
-                return
             if h == 0:
                 z_rows[d] = tile([P, H], BF16, "z_rows%d" % d)
             dst = z_rows[d][:].rearrange("v (u h q) -> v u h q", u=2, h=2)[:, :, h, :]
@@ -225,12 +221,12 @@ def tile_picked_yfism_lin_p_kernel(
                 nc.scalar.activation(dst.rearrange("v u (p s) -> v u p s", s=2), dealt(direct[:, 0:HALF]), COPY, scale=factor)
                 return
             src = others[d, h][:].rearrange("v (u q) -> v u q", u=2)
-            if (d, h) == (3, 0):
+            if h == 0 and d % 2 == 1:
                 nc.gpsimd.tensor_scalar(dst, src, factor, 0.0, MULT, ADD)
             else:
                 nc.scalar.activation(dst, src, COPY, scale=factor)
 
-        z_cols = {}
+        z_cols = {d: tile([P, PASS], BF16, "z_cols%d" % d)[:] for d in range(D)}
         turned = {}
 
         def turn(d):
@@ -240,17 +236,13 @@ def tile_picked_yfism_lin_p_kernel(
                 nc.tensor.transpose(turned[d][:, u * P : (u + 1) * P], pairs[:, u * P : (u + 1) * P], ident[:])
 
         def copy_turned(d):
-            z_cols[d] = tile([P, P * PACK], BF16, "z_cols%d" % d)
             nc.scalar.copy(
-                z_cols[d][:].bitcast(F32).rearrange("p (c u) -> p c u", u=2),
+                z_cols[d].bitcast(F32).rearrange("p (c u) -> p c u", u=2),
                 turned[d][:, 0 : 2 * P].rearrange("p (u c) -> p c u", u=2),
             )
 
         out_tiles = out.rearrange("(v d) g -> d v g", d=D)
         z_mx = {}
-
-        def quantise_z(d):
-            z_mx[d] = quantise("z%d" % d, z_cols[d], P)
 
         COLS = R // 2
 
@@ -258,8 +250,8 @@ def tile_picked_yfism_lin_p_kernel(
             scores = bank(on_bank, "scores%d%d" % (d, a))
             nc.tensor.matmul_mx(
                 out=scores[:, 0 : b - a],
-                lhsT=z_mx[d][0][:].bitcast(FP8X4),
-                lhsT_scale=z_mx[d][1][:],
+                lhsT=z_mx[d][0].bitcast(FP8X4),
+                lhsT_scale=z_mx[d][1],
                 rhs=v_picked[:, a:b].bitcast(FP8X4),
                 rhs_scale=v_plane[:, a:b],
                 start=True,
@@ -279,9 +271,7 @@ def tile_picked_yfism_lin_p_kernel(
         near = combine("pair01", y0, y(1, 0), ADD)
         others[0, 0] = combine("others00", far, y(1, 0), ADD)
         others[2, 0] = combine("others20", near, y(3, 0), ADD)
-        last_others = tile([P, H], F32, "others1")
-        last_halves = last_others[:].rearrange("v (u h q) -> v h u q", u=2, h=2)
-        nc.gpsimd.tensor_tensor(last_halves[:, 0], by_u(y0), by_u(far), ADD)
+        others[1, 0] = combine_copies("others10", y0, far, ADD)
         others[3, 0] = combine_copies("others30", y2, near, ADD)
 
         whole = combine("whole", copy_y(0, 1), direct[:, 0:HALF], ADD)
@@ -289,19 +279,18 @@ def tile_picked_yfism_lin_p_kernel(
         for d in (3, 1):
             for o in range(2):
                 project(o, d, second[o], 0, y(d, 1), d == 3, d == 1)
-        for d in (2, 3):
+        for d in (2, 3, 1):
             others[d, 1] = combine("others%d1" % d, whole, y(d, 1), SUB)
-        nc.vector.tensor_tensor(
-            last_halves[:, 1].rearrange("v u (p s) -> v u p s", s=2), shaped(whole), dealt(y(1, 1)), SUB
-        )
         v_picked = tile([P, R], U32, "v_picked", tag="copy01")
         nc.vector.tensor_copy(v_picked[:], v_win[:].indirect(items_sb[:]))
-        for d, h in ((3, 0), (0, 0), (2, 0), (0, 1), (2, 1), (3, 1), (1, None)):
+        for d, h in ((3, 0), (1, 0), (0, 0), (2, 0), (0, 1), (2, 1), (3, 1), (1, 1)):
             apply_norm(d, h)
         for d in (0, 2, 3, 1):
             turn(d)
             copy_turned(d)
-            quantise_z(d)
+        z_mx[0] = [part[:] for part in quantise("z0", z_cols[0], P)]
+        for d in (2, 3, 1):
+            z_mx[d] = [part[:] for part in quantise("z%d" % d, z_cols[d], P)]
         for d, on_bank in ((0, 7), (2, 6), (3, 3)):
             store(d, 0, score(d, 0, R, on_bank))
         for a, on_bank in ((0, 2), (COLS, 4)):

@@ -138,7 +138,7 @@ def tile_picked_yfism_lin_p_kernel(
             nc.vector.tensor_copy(by_item(x_picked[o]), x_win[o][:].indirect(offs_sb[:]))
 
         alone = {(d, 0): bank(b, "y%d0" % d) for d, b in ((2, 4), (3, 5), (0, 0), (1, 1))}
-        alone.update({(d, 1): bank(b, "y%d1" % d) for d, b in ((0, 2), (2, 3))})
+        alone.update({(d, 1): bank(b, "y%d1" % d) for d, b in ((0, 2),)})
         paired = []
         direct = bank(6, "direct")
 
@@ -166,7 +166,6 @@ def tile_picked_yfism_lin_p_kernel(
             project(o, 0, w_mx, first, y(0, 1), True, True)
             for d in (1, 2, 3):
                 project(o, d, w_mx, first, direct[:, 0:HALF], d == 1, d == 3)
-            project(o, 2, w_mx, first, y(2, 1), True, True)
 
         w_mx00 = quantise("w00", w_bf0[0], HALF)
         gather_x(0)
@@ -230,7 +229,7 @@ def tile_picked_yfism_lin_p_kernel(
         turned = {}
 
         def turn(d):
-            turned[d] = bank((4, 5, 1, 0)[d], "turned%d" % d)
+            turned[d] = bank((3, 5, 1, 0)[d], "turned%d" % d)
             pairs = z_rows[d][:].bitcast(F32)
             for u in range(2):
                 nc.tensor.transpose(turned[d][:, u * P : (u + 1) * P], pairs[:, u * P : (u + 1) * P], ident[:])
@@ -266,6 +265,9 @@ def tile_picked_yfism_lin_p_kernel(
             nc.sync.dma_start(out_tiles[d, :, a:b], result[:])
 
         y2 = copy_y(2, 0)
+        alone[2, 1] = bank(4, "y21")
+        for o in range(2):
+            project(o, 2, second[o], 0, y(2, 1), True, True)
         y0 = copy_y(0, 0)
         far = combine("pair23", y2, y(3, 0), ADD)
         near = combine("pair01", y0, y(1, 0), ADD)
@@ -291,7 +293,7 @@ def tile_picked_yfism_lin_p_kernel(
         z_mx[0] = [part[:] for part in quantise("z0", z_cols[0], P)]
         for d in (2, 3, 1):
             z_mx[d] = [part[:] for part in quantise("z%d" % d, z_cols[d], P)]
-        for d, on_bank in ((0, 7), (2, 6), (3, 3)):
+        for d, on_bank in ((0, 7), (2, 6), (3, 4)):
             store(d, 0, score(d, 0, R, on_bank))
-        for a, on_bank in ((0, 2), (COLS, 4)):
+        for a, on_bank in ((0, 2), (COLS, 3)):
             store(1, a, score(1, a, a + COLS, on_bank))

from contextlib import ExitStack

import concourse.mybir as mybir
from concourse.masks import make_identity

K, T, S, H, G, R, D = 1024, 2048, 512, 512, 2048, 512, 4
FLOPS = 2 * K * H * S + 2 * H * S * R

F32 = mybir.dt.float32
BF16 = mybir.dt.bfloat16
I32 = mybir.dt.int32
U32 = mybir.dt.uint32
U16 = mybir.dt.uint16
U8 = mybir.dt.uint8
FP8X4 = mybir.dt.float8_e4m3fn_x4
COPY = mybir.ActivationFunctionType.Copy
MULT = mybir.AluOpType.mult
ADD = mybir.AluOpType.add
SUB = mybir.AluOpType.subtract

P = 128
PACK = 4
PASS = P * PACK
BANK = 512
QUAD = 32
BLOCKS = PASS // 32
HALF = H // 2
X_ROWS = P - 2 * BLOCKS
V_ROWS = 2 * QUAD - BLOCKS
SCALAR_COLS = 96


def tile_picked_yfism_lin_p_kernel(
    tc, x_words, x_scales, w1, norm, v_words, v_scales, bias, offs, items, out
):
    nc = tc.nc
    with ExitStack() as ctx:
        sb = ctx.enter_context(tc.tile_pool(name="sb", bufs=1))
        shared = ctx.enter_context(tc.tile_pool(name="shared", bufs=1))
        ps = ctx.enter_context(tc.psum_pool(name="ps", bufs=1))

        def bank(b, name):
            return ps.tile([P, BANK], F32, name=name, tag="bank%d" % b)

        def tile(shape, dtype, name, tag=None):
            return sb.tile(shape, dtype, name=name, tag=tag or name, align_bytes=64)

        offs_sb = tile([P, S // 16], U16, "offs_sb")
        items_sb = tile([P, R // 16], U16, "items_sb")
        x_scale_win = tile([P, T], U8, "x_scale_win")
        v_scale_win = tile([P, G], U8, "v_scale_win")
        bias_win = shared.tile([P, G], F32, name="bias_win", align_bytes=64, offset=0)
        nc.gpsimd.memset(x_scale_win[0:X_ROWS, :].bitcast(I32), 0)
        nc.vector.memset(bias_win[0 : P - 1, :], 0.0)
        x_plane = tile([P, S], U8, "x_plane")
        nc.gpsimd.memset(x_plane[:].bitcast(I32), 0)
        nc.gpsimd.memset(v_scale_win[0:V_ROWS, :].bitcast(I32), 0)
        nc.gpsimd.memset(v_scale_win[V_ROWS + BLOCKS : P, :].bitcast(I32), 0)
        v_plane = tile([P, R], U8, "v_plane")
        nc.gpsimd.memset(v_plane[:].bitcast(I32), 0)
        ident = tile([P, P], F32, "ident")
        make_identity(nc, ident[:])

        def load_words(name, tag, words):
            window = tile([P, T], U32, name, tag=tag)
            nc.sync.dma_start(window[:].bitcast(I32), words.rearrange("p n t -> p (n t)").bitcast(I32))
            return window

        nc.sync.dma_start(offs_sb[:], offs)
        nc.scalar.dma_start(x_scale_win[X_ROWS:P, :].bitcast(I32), x_scales.rearrange("o q n -> (o q) n").bitcast(I32))
        nc.scalar.dma_start(v_scale_win[V_ROWS : V_ROWS + BLOCKS, :].bitcast(I32), v_scales[0].bitcast(I32))
        nc.scalar.dma_start(bias_win[P - 1 : P, :], bias[0:1, :])
        nc.sync.dma_start(items_sb[:], items)
        w_raw0 = tile([P, PACK, H], F32, "w_raw0")
        nc.sync.dma_start(w_raw0[:].rearrange("p j c -> p (j c)"), w1[0:PASS, :].rearrange("(p j) c -> p (j c)", j=PACK))
        x_win = [load_words("x_win0", None, x_words[0])]

        def by_item(picked):
            return picked[:].rearrange("p (d v) -> p v d", d=D)

        x_scale_picked = tile([P, S], U8, "x_scale_picked")
        nc.vector.tensor_copy(by_item(x_scale_picked), x_scale_win[:].indirect(offs_sb[:]))
        v_scale_picked = tile([P, R], U8, "v_scale_picked")
        nc.vector.tensor_copy(v_scale_picked[:], v_scale_win[:].indirect(items_sb[:]))
        bias_picked = tile([P, R], F32, "bias_picked")
        nc.vector.tensor_copy(bias_picked[:], bias_win[:].indirect(items_sb[:]))

        def place_scales(plane, a, picked, first_row):
            for q in range(P // QUAD):
                rows = picked[first_row + 4 * q : first_row + 4 * q + 4, :]
                nc.sync.dma_start(plane[QUAD * q + a : QUAD * q + a + 4, :].bitcast(I32), rows.bitcast(I32))

        place_scales(x_plane, 0, x_scale_picked, X_ROWS)
        x_win.append(load_words("x_win1", "x_scale_win", x_words[1]))
        place_scales(x_plane, 4, x_scale_picked, X_ROWS + BLOCKS)
        w_raw1 = []
        w_raw1.append(tile([P, PACK, HALF], F32, "w_raw10", tag="v_scale_win"))
        w_raw1.append(shared.tile([P, PACK, HALF], F32, name="w_raw11", align_bytes=64, offset=0))
        for h in range(2):
            nc.sync.dma_start(w_raw1[h][:], w1[PASS:K, h * HALF : (h + 1) * HALF].rearrange("(p j) c -> p j c", j=PACK))
        norm_col = shared.tile([P, D], F32, name="norm_col", align_bytes=64, offset=4 * PACK * HALF)
        nc.sync.dma_start(norm_col[:], norm[0, :].rearrange("(v d) -> v d", d=D))

        bias_turned = bank(7, "bias_turned")
        for c in range(R // P):
            nc.tensor.transpose(bias_turned[:, c * P : (c + 1) * P], bias_picked[:, c * P : (c + 1) * P], ident[:])
        v_win = load_words("v_win", "bias_picked", v_words[0])
        place_scales(v_plane, 0, v_scale_picked, V_ROWS)

        def round_w(copy, w_bf, raw, a, b):
            dst = w_bf[:, PACK * a : PACK * b]
            copy(dst.rearrange("p (c i t) -> p c t i", i=4, t=PACK), raw[:, :, a:b].rearrange("p t (c i) -> p c t i", i=4))

        def quantise(name, values, cols):
            codes = tile([P, cols], U32, name + "_codes")
            scales = tile([P, cols], U8, name + "_scales")
            nc.vector.quantize_mx(codes[:].bitcast(FP8X4), scales[:], values[:])
            return codes, scales

        w_bf0 = [tile([P, PACK * HALF], BF16, "w_bf0%d" % h) for h in range(2)]
        for h in range(2):
            round_w(nc.scalar.copy, w_bf0[h], w_raw0[:, :, h * HALF : (h + 1) * HALF], 0, HALF)

        bias_col = tile([P, R // P], F32, "bias_col", tag="w_raw0")
        nc.scalar.copy(bias_col[:], bias_turned[:, P - 1 : BANK : P])
        bias_spread = bank(6, "bias_spread")
        for c in range(R // P):
            nc.tensor.transpose(
                bias_spread[:, c * P : (c + 1) * P], bias_col[:, c : c + 1].to_broadcast([P, P]), ident[:]
            )
        bias_all = tile([P, R], F32, "bias_all")
        nc.scalar.copy(bias_all[:], bias_spread[:])

        x_picked = []

        def gather_x(o):
            x_picked.append(tile([P, S], U32, "x_picked%d" % o))
            nc.vector.tensor_copy(by_item(x_picked[o]), x_win[o][:].indirect(offs_sb[:]))

        alone = {(d, 0): bank(b, "y%d0" % d) for d, b in ((2, 4), (3, 5), (0, 0), (1, 1))}
        alone.update({(d, 1): bank(b, "y%d1" % d) for d, b in ((0, 2),)})
        paired = []
        direct = bank(6, "direct")

        def y(d, h):
            if (d, h) in alone:
                return alone[d, h][:, 0:HALF]
            return paired[0][:, d // 2 * HALF : (d // 2 + 1) * HALF]

        def project(o, d, w_mx, first, cols, opens, closes):
            nc.tensor.matmul_mx(
                out=cols,
                lhsT=x_picked[o][:, d * P : (d + 1) * P].bitcast(FP8X4),
                lhsT_scale=x_plane[4 * o : P, d * P : (d + 1) * P],
                rhs=w_mx[0][:, first : first + HALF].bitcast(FP8X4),
                rhs_scale=w_mx[1][:, first : first + HALF],
                start=(o == 0 and opens),
                stop=(o == 1 and closes),
            )

        def project_half(o, h, w_mx, first):
            if h == 0:
                for d in (2, 3, 0, 1):
                    project(o, d, w_mx, first, y(d, 0), True, True)
                return
            project(o, 0, w_mx, first, y(0, 1), True, True)
            for d in (1, 2, 3):
                project(o, d, w_mx, first, direct[:, 0:HALF], d == 1, d == 3)

        w_mx00 = quantise("w00", w_bf0[0], HALF)
        gather_x(0)
        project_half(0, 0, w_mx00, 0)
        second = [quantise("w01", w_bf0[1], HALF)]
        project_half(0, 1, second[0], 0)
        gather_x(1)
        for h in range(2):
            w_bf = tile([P, PACK * HALF], BF16, "w_bf1%d" % h, tag="w_raw0" if h == 0 else None)
            round_w(nc.scalar.copy, w_bf, w_raw1[h], 0, SCALAR_COLS)
            round_w(nc.vector.tensor_copy, w_bf, w_raw1[h], SCALAR_COLS, HALF)
            w_mx = quantise("w1%d" % h, w_bf, HALF)
            project_half(1, h, w_mx, 0)
        second.append(w_mx)

        def dealt(bank_cols):
            return bank_cols.rearrange("v (p u s) -> v u p s", u=2, s=2)

        def shaped(t):
            return t[:].rearrange("v (u p s) -> v u p s", u=2, s=2)

        def by_u(t):
            return t[:].rearrange("v (u q) -> v u q", u=2)

        def half_tile(name, tag=None):
            return tile([P, HALF], F32, name, tag=tag)

        def copy_y(d, h):
            copy = half_tile("copy%d%d" % (d, h))
            nc.scalar.copy(shaped(copy), dealt(y(d, h)))
            return copy

        def combine(name, sbuf, psum, op, tag=None):
            made = half_tile(name, tag)
            nc.vector.tensor_tensor(shaped(made), shaped(sbuf), dealt(psum), op)
            return made

        def combine_copies(name, left, right, op):
            made = half_tile(name)
            nc.gpsimd.tensor_tensor(made[:], left[:], right[:], op)
            return made

        others = {}
        z_rows = {}

        def apply_norm(d, h):
            factor = norm_col[:, d : d + 1]
            if h == 0:
                z_rows[d] = tile([P, H], BF16, "z_rows%d" % d)
            dst = z_rows[d][:].rearrange("v (u h q) -> v u h q", u=2, h=2)[:, :, h, :]
            if (d, h) == (0, 1):
                nc.scalar.activation(dst.rearrange("v u (p s) -> v u p s", s=2), dealt(direct[:, 0:HALF]), COPY, scale=factor)
                return
            src = others[d, h][:].rearrange("v (u q) -> v u q", u=2)
            if h == 0 and d % 2 == 1:
                nc.gpsimd.tensor_scalar(dst, src, factor, 0.0, MULT, ADD)
            else:
                nc.scalar.activation(dst, src, COPY, scale=factor)

        z_cols = {d: tile([P, PASS], BF16, "z_cols%d" % d)[:] for d in range(D)}
        turned = {}

        def turn(d):
            turned[d] = bank((3, 5, 1, 0)[d], "turned%d" % d)
            pairs = z_rows[d][:].bitcast(F32)
            for u in range(2):
                nc.tensor.transpose(turned[d][:, u * P : (u + 1) * P], pairs[:, u * P : (u + 1) * P], ident[:])

        def copy_turned(d):
            nc.scalar.copy(
                z_cols[d].bitcast(F32).rearrange("p (c u) -> p c u", u=2),
                turned[d][:, 0 : 2 * P].rearrange("p (u c) -> p c u", u=2),
            )

        out_tiles = out.rearrange("(v d) g -> d v g", d=D)
        z_mx = {}

        COLS = R // 2

        def score(d, a, b, on_bank):
            scores = bank(on_bank, "scores%d%d" % (d, a))
            nc.tensor.matmul_mx(
                out=scores[:, 0 : b - a],
                lhsT=z_mx[d][0].bitcast(FP8X4),
                lhsT_scale=z_mx[d][1],
                rhs=v_picked[:, a:b].bitcast(FP8X4),
                rhs_scale=v_plane[:, a:b],
                start=True,
                stop=True,
            )
            return scores[:, 0 : b - a]

        def store(d, a, scores):
            b = a + scores.shape[1]
            result = tile([P, b - a], F32, "result%d%d" % (d, a))
            nc.vector.tensor_tensor(result[:], scores, bias_all[:, a:b], ADD)
            nc.sync.dma_start(out_tiles[d, :, a:b], result[:])

        y2 = copy_y(2, 0)
        alone[2, 1] = bank(4, "y21")
        for o in range(2):
            project(o, 2, second[o], 0, y(2, 1), True, True)
        y0 = copy_y(0, 0)
        far = combine("pair23", y2, y(3, 0), ADD)
        near = combine("pair01", y0, y(1, 0), ADD)
        others[0, 0] = combine("others00", far, y(1, 0), ADD)
        others[2, 0] = combine("others20", near, y(3, 0), ADD)
        others[1, 0] = combine_copies("others10", y0, far, ADD)
        others[3, 0] = combine_copies("others30", y2, near, ADD)

        whole = combine("whole", copy_y(0, 1), direct[:, 0:HALF], ADD)
        paired.append(bank(2, "y_odd"))
        for d in (3, 1):
            for o in range(2):
                project(o, d, second[o], 0, y(d, 1), d == 3, d == 1)
        for d in (2, 3, 1):
            others[d, 1] = combine("others%d1" % d, whole, y(d, 1), SUB)
        v_picked = tile([P, R], U32, "v_picked", tag="copy01")
        nc.vector.tensor_copy(v_picked[:], v_win[:].indirect(items_sb[:]))
        for d, h in ((3, 0), (1, 0), (0, 0), (2, 0), (0, 1), (2, 1), (3, 1), (1, 1)):
            apply_norm(d, h)
        for d in (0, 2, 3, 1):
            turn(d)
            copy_turned(d)
        z_mx[0] = [part[:] for part in quantise("z0", z_cols[0], P)]
        for d in (2, 3, 1):
            z_mx[d] = [part[:] for part in quantise("z%d" % d, z_cols[d], P)]
        for d, on_bank in ((0, 7), (2, 6), (3, 4)):
            store(d, 0, score(d, 0, R, on_bank))
        for a, on_bank in ((0, 2), (COLS, 3)):
            store(1, a, score(1, a, a + COLS, on_bank))
